import numpy as np
import ml_dtypes


def mxq(x, axis, fmt="e4m3"):
    dtype, down = {"e4m3": (ml_dtypes.float8_e4m3fn, 7), "e5m2": (ml_dtypes.float8_e5m2, 14)}[fmt]
    v = np.moveaxis(np.asarray(x, np.float32).astype(ml_dtypes.bfloat16).astype(np.float64), axis, -1)
    blocks = v.reshape(v.shape[:-1] + (-1, 32))
    amax = np.abs(blocks).max(-1, keepdims=True)
    byte = np.maximum(np.where(amax > 0, np.frexp(amax)[1] - 1 + 127, 0) - down, 1)
    scale = np.exp2(byte - 127.0)
    codes = (blocks / scale).astype(np.float32).astype(dtype).astype(np.float64)
    return np.moveaxis((codes * scale).reshape(v.shape), -1, axis)


WIDE = False


def mx_kscale(k):
    if not WIDE:
        return np.ones(k)
    levels = np.array([10, -10, 5, -5, 0])
    if k % 512:
        return np.exp2(np.random.permutation(np.resize(levels, k // 32))).repeat(32)
    a = np.empty((k // 512, 16))
    for p in range(k // 512):
        a[p, :8] = np.random.permutation(np.resize(levels, 8))
        for g in range(8):
            far = levels[np.abs(levels - a[p, g]) >= 10]
            a[p, g + 8] = far[np.random.randint(len(far))]
    return np.exp2(a.ravel()).repeat(32)


BF16 = ml_dtypes.bfloat16


def bf(x):
    return np.asarray(x, np.float32).astype(BF16)


def f64(x):
    return np.asarray(x).astype(np.float64)


E2M1 = np.array([0.0, 0.5, 1.0, 1.5, 2.0, 3.0, 4.0, 6.0, -0.0, -0.5, -1.0, -1.5, -2.0, -3.0, -4.0, -6.0])


def pack_weight(w, fmt):
    k, n = w.shape
    w = f64(bf(w)).reshape(k // 32, 32, n)
    amax = np.abs(w).max(1)
    if fmt == "e4m3":
        byte = np.frexp(amax)[1] - 1 + 127 - 7
    else:
        mant, ex = np.frexp(amax / 6.0)
        byte = np.where(mant > 0.5, ex, ex - 1) + 127
    byte = np.clip(np.where(amax > 0, byte, 1), 1, 254)
    scaled = (w * np.exp2(127.0 - byte)[:, None, :]).reshape(k, n).astype(np.float32)
    by_word = np.ascontiguousarray(scaled.reshape(k // 512, 128, 4, n).transpose(0, 1, 3, 2))
    if fmt == "e4m3":
        words = by_word.astype(ml_dtypes.float8_e4m3fn).view(np.uint8)
    else:
        c = by_word.astype(ml_dtypes.float4_e2m1fn).view(np.uint8) & 0xF
        words = c[..., 0::2] | (c[..., 1::2] << 4)
    return np.ascontiguousarray(words), np.ascontiguousarray(byte.astype(np.uint8).reshape(k // 512, 16, n))


def unpack_weight(words, scales, fmt):
    g, p, n, _ = words.shape
    if fmt == "e4m3":
        vals = np.ascontiguousarray(words).view(ml_dtypes.float8_e4m3fn).astype(np.float64)
    else:
        nib = np.empty((g, p, n, 4), np.uint8)
        nib[..., 0::2] = words & 0xF
        nib[..., 1::2] = words >> 4
        vals = E2M1[nib]
    vals = vals * np.repeat(np.exp2(scales.astype(np.float64) - 127.0), 8, axis=1)[..., None]
    return vals.transpose(0, 1, 3, 2).reshape(g * 512, n)
def pack4(w):
    words, scales = pack_weight(w, "e2m1")
    return words.reshape(words.shape[0], 128, -1), scales


def unpack4(words, scales):
    return unpack_weight(words.reshape(words.shape[0], 128, -1, 2), scales, "e2m1")


def planes(Y):
    n, m = Y.shape
    b = f64(bf(Y)).reshape(n // 32, 32, m)
    amax = np.abs(b).max(1)
    byte = np.clip(np.where(amax > 0, np.frexp(amax)[1] - 1 + 127 - 7, 1), 1, 254)
    codes = (b * np.exp2(127.0 - byte)[:, None, :]).reshape(n, m).astype(np.float32).astype(ml_dtypes.float8_e4m3fn).view(np.uint8)
    words = codes.reshape(n // 512, 128, 4, m).transpose(0, 1, 3, 2)
    return np.ascontiguousarray(words), np.ascontiguousarray(byte.astype(np.uint8).reshape(n // 512, 16, m))


U, I, F = 768, 2048, 1024
DENSITY, ALPHA = 0.1, 2.0

def setup_inputs():
    s = mx_kscale(I)[:, None]
    noise = np.random.randn
    spread = np.exp(0.7 * noise(F))
    pref = 1.0 * (np.random.rand(I, U) < DENSITY)
    conf = 1.0 + ALPHA * pref * np.random.exponential(size=(I, U))
    e = conf * (pref - 0.3 * noise(I, U))
    a = 0.6 * noise(I, F) * spread / np.sqrt(I)
    b = 0.6 * noise(I, F) * spread / np.sqrt(I)
    d = 0.4 * noise(I, F) * spread / np.sqrt(I)
    e_words, e_scales = pack_weight(e * s, "e4m3")
    a_words, a_scales = pack4(a / s)
    b_words, b_scales = pack_weight(b / s, "e4m3")
    return {"e_words": e_words, "e_scales": e_scales,
            "a_words": a_words, "a_scales": a_scales,
            "b_words": b_words, "b_scales": b_scales,
            "d": bf(d / s),
            "gain": bf(0.6 + 0.3 * noise(U, F)),
            "x": bf(noise(U, F) * spread)}

def reference(e_words, e_scales, a_words, a_scales, b_words, b_scales, d, gain, x):
    e = unpack_weight(e_words, e_scales, "e4m3")
    ea = e.T @ unpack4(a_words, a_scales)
    eb = e.T @ unpack_weight(b_words, b_scales, "e4m3")
    ed = e.T @ mxq(f64(d), 0, "e4m3")
    y = f64(x) - (ea + f64(gain) * eb + ed)
    Y = y.T
    words, scales = planes(Y)
    return y, words, scales

@@ -1,0 +1,354 @@
+from contextlib import ExitStack
+
+import concourse.mybir as mybir
+from concourse.masks import make_identity
+
+USERS, ITEMS, FACTORS = 768, 2048, 1024
+FLOPS = 3 * 2 * USERS * ITEMS * FACTORS
+
+F32 = mybir.dt.float32
+BF16 = mybir.dt.bfloat16
+I32 = mybir.dt.int32
+U32 = mybir.dt.uint32
+U8 = mybir.dt.uint8
+FP8X4 = mybir.dt.float8_e4m3fn_x4
+FP4X4 = mybir.dt.float4_e2m1fn_x4
+MULT = mybir.AluOpType.mult
+SUBTRACT = mybir.AluOpType.subtract
+
+P = 128
+PACK = 4
+K_PASS = P * PACK
+PASSES = ITEMS // K_PASS
+TILES = USERS // P
+HALF = 512
+HALVES = FACTORS // HALF
+QUADRANTS = 4
+ALIGN = 256
+
+
+def tile_implicit_als_user_gradient_k3_kernel(
+    tc, e_words, e_scales, a_words, a_scales, b_words, b_scales, d, gain, x, out_0, out_1, out_2
+):
+    nc = tc.nc
+    with ExitStack() as ctx:
+        keep = ctx.enter_context(tc.tile_pool(name="keep", bufs=1))
+        psum = ctx.enter_context(tc.psum_pool(name="psum", bufs=1))
+        ctx.enter_context(tc.manual_schedule())
+
+        def sb(name, shape, dtype, tag="", bufs=None):
+            return keep.tile(shape, dtype, name=name, tag=tag, bufs=bufs, align_bytes=ALIGN)
+
+        def bank(index, name, shape):
+            return psum.tile(shape, F32, name=name, tag="bank%d" % index)
+
+        e_code = [sb("e_code%d" % g, [P, USERS], U32) for g in range(PASSES)]
+        e_scale_first = sb("e_scale_first", [P, USERS], U8)
+        e_scale_rest = sb("e_scale_rest", [P, PASSES - 1, USERS], U8)
+        b_code = [[sb("b_code%d_%d" % (h, g), [P, HALF], U32) for g in range(PASSES)] for h in range(HALVES)]
+        b_scale = sb("b_scale", [P, FACTORS], U8)
+        a_code = [sb("a_code%d" % g, [P, 2 * FACTORS], U8) for g in range(PASSES)]
+        a_scale = sb("a_scale", [P, PASSES, FACTORS], U8)
+        d_raw = [sb("d_raw%d" % g, [P, PACK, FACTORS], BF16) for g in range(PASSES)]
+        d_code = [[sb("d_code%d_%d" % (h, g), [P, HALF], U32) for g in range(PASSES)] for h in range(HALVES)]
+        d_scale = [[sb("d_scale%d_%d" % (h, g), [P, HALF], U8) for g in range(PASSES)] for h in range(HALVES)]
+        gain_sb = [sb("gain%d" % t, [P, FACTORS], BF16) for t in range(TILES)]
+        x_sb = [sb("x%d" % t, [P, FACTORS], BF16) for t in range(TILES)]
+        rest = [[sb("rest%d_%d" % (h, t), [P, HALF], F32) for t in range(TILES)] for h in range(HALVES)]
+        y_pairs = [[sb("y_pairs%d_%d" % (h, t), [P, HALF], BF16) for t in range(TILES)] for h in range(HALVES)]
+        y_turned = [sb("y_turned%d" % h, [P, USERS * PACK], BF16) for h in range(HALVES)]
+        y_code = [sb("y_code%d" % h, [P, USERS], U32) for h in range(HALVES)]
+        y_scale = [sb("y_scale%d" % h, [P, USERS], U8) for h in range(HALVES)]
+        ident = sb("ident", [P, P], F32)
+
+        def users(t, count=1):
+            return slice(t * P, (t + count) * P)
+
+        def half(h):
+            return slice(h * HALF, (h + 1) * HALF)
+
+        def live(q, rows=4):
+            return slice(32 * q, 32 * q + rows)
+
+        def scale_rows(q):
+            return slice(4 * q, 4 * q + 4)
+
+        def load(dst, src):
+            nc.sync.dma_start(out=dst, in_=src)
+
+        def load_e(g, t0, count):
+            src = e_words[g].rearrange("p n t -> p (n t)").bitcast(I32)
+            load(e_code[g][:, users(t0, count)].bitcast(I32), src[:, users(t0, count)])
+
+        def load_b(h, g):
+            src = b_words[g].rearrange("p n t -> p (n t)").bitcast(I32)
+            load(b_code[h][g][:].bitcast(I32), src[:, half(h)])
+
+        def load_e_scale_first(q):
+            load(e_scale_first[live(q), :].bitcast(I32), e_scales[0, scale_rows(q), :].bitcast(I32))
+
+        def load_e_scale_rest(q):
+            src = e_scales[1:PASSES, scale_rows(q), :].rearrange("g r n -> r g n")
+            load(e_scale_rest[live(q), :, :].bitcast(I32), src.bitcast(I32))
+
+        def load_b_scale(q):
+            load(b_scale[live(q, 16), :].bitcast(I32), b_scales[:, scale_rows(q), :].bitcast(I32))
+
+        def load_a_scale(q):
+            src = a_scales[:, scale_rows(q), :].rearrange("g r n -> r g n")
+            load(a_scale[live(q), :, :].bitcast(I32), src.bitcast(I32))
+
+        def load_a(g):
+            load(a_code[g][:].bitcast(I32), a_words[g].bitcast(I32))
+
+        def load_d(g):
+            load(d_raw[g][:], d[g * K_PASS:(g + 1) * K_PASS, :].rearrange("(p j) f -> p j f", j=PACK))
+
+        nc.vector.memset(e_scale_first[:].bitcast(I32), 0)
+        nc.vector.memset(b_scale[:].bitcast(I32), 0)
+        nc.vector.memset(e_scale_rest[:].bitcast(I32), 0)
+        nc.vector.memset(a_scale[:].bitcast(I32), 0)
+        nc.vector.memset(ident[:], 0.0)
+        make_identity(nc, ident[:], nomemset=True)
+
+        load_e_scale_first(0)
+        load_e_scale_first(2)
+        load_b(0, 0)
+        load_e(0, 0, 3)
+        load_e_scale_first(1)
+        load_e_scale_first(3)
+        for q in range(QUADRANTS):
+            load_b_scale(q)
+        load_e(0, 3, 3)
+        for q in range(QUADRANTS):
+            load_e_scale_rest(q)
+        for g in range(1, PASSES):
+            load_b(0, g)
+            load_e(g, 0, TILES)
+        for g in range(PASSES):
+            load_b(1, g)
+        for t in range(TILES):
+            load(gain_sb[t][:], gain[users(t), :])
+        for q in range(QUADRANTS):
+            load_a_scale(q)
+        load_a(0)
+        load_d(0)
+        for g in range(1, PASSES):
+            load_a(g)
+        for g in range(1, PASSES):
+            load_d(g)
+        for t in range(TILES):
+            load(x_sb[t][:], x[users(t), :])
+
+        def mx_pass(acc, t, g, rhs, rhs_scale, start, stop):
+            e_scale = e_scale_first[:, users(t)] if g == 0 else e_scale_rest[:, g - 1, users(t)]
+            nc.tensor.matmul_mx(
+                out=acc[:],
+                lhsT=e_code[g][:, users(t)].bitcast(FP8X4),
+                lhsT_scale=e_scale,
+                rhs=rhs,
+                rhs_scale=rhs_scale,
+                start=start,
+                stop=stop,
+            )
+
+        def pass_b(acc, h, t, g):
+            mx_pass(acc, t, g, b_code[h][g][:].bitcast(FP8X4), b_scale[4 * g:P, half(h)], g == 0, g == PASSES - 1)
+
+        def pass_a(acc, h, t, g):
+            rhs = a_code[g][:, 2 * h * HALF:2 * (h + 1) * HALF].bitcast(FP4X4)
+            mx_pass(acc, t, g, rhs, a_scale[:, g, half(h)], g == 0, False)
+
+        def pass_d(acc, h, t, g):
+            mx_pass(acc, t, g, d_code[h][g][:].bitcast(FP8X4), d_scale[h][g][:], False, g == PASSES - 1)
+
+        grouped = {}
+
+        def interleave_d(h, g, on_vector):
+            dst = sb("d_grouped%d_%d" % (h, g), [P, HALF, PACK], BF16, tag="d_grouped", bufs=4)
+            grouped[h, g] = dst
+            src = d_raw[g][:, :, half(h)].rearrange("p j c -> p c j")
+            if on_vector:
+                nc.vector.tensor_copy(out=dst[:], in_=src)
+            else:
+                nc.scalar.copy(out=dst[:], in_=src)
+
+        def quantise_d(h, g):
+            nc.vector.quantize_mx(
+                out=d_code[h][g][:].bitcast(FP8X4),
+                scales=d_scale[h][g][:],
+                in_=grouped[h, g][:].rearrange("p c j -> p (c j)"),
+            )
+
+        acc_b, acc_ad, y_sb, turn = {}, {}, {}, {}
+
+        def weigh(h, t):
+            nc.vector.tensor_tensor(out=rest[h][t][:], in0=acc_b[h, t][:], in1=gain_sb[t][:, half(h)], op=MULT)
+
+        def subtract_from_x(h, t):
+            nc.vector.tensor_tensor(out=rest[h][t][:], in0=x_sb[t][:, half(h)], in1=rest[h][t][:], op=SUBTRACT)
+
+        def finish(h, t):
+            y_sb[h, t] = sb("y%d_%d" % (h, t), [P, HALF], F32, tag="y", bufs=TILES)
+            nc.vector.tensor_tensor(out=y_sb[h, t][:], in0=rest[h][t][:], in1=acc_ad[h, t][:], op=SUBTRACT)
+
+        def pair_view(ap):
+            return ap.rearrange("u (p e i) -> u e p i", e=2, i=2)
+
+        def pairs_out(h, t):
+            return y_pairs[h][t][:].rearrange("u (e p i) -> u e p i", e=2, i=2)
+
+        def round_y(h, t):
+            nc.scalar.copy(out=pairs_out(h, t), in_=pair_view(y_sb[h, t][:]))
+
+        def finish_rounded(h, t):
+            nc.vector.tensor_tensor(
+                out=pairs_out(h, t), in0=pair_view(rest[h][t][:]), in1=pair_view(acc_ad[h, t][:]), op=SUBTRACT
+            )
+
+        def transpose_y(h, t0, count, bank_index):
+            turn[h, t0] = bank(bank_index, "turn%d_%d" % (h, t0), [P, count, 2, P])
+            for j in range(count):
+                words = y_pairs[h][t0 + j][:].bitcast(F32)
+                for e in range(2):
+                    nc.tensor.transpose(turn[h, t0][:, j, e, :], words[:, e * P:(e + 1) * P], ident[:])
+
+        def copy_turned(h, t0, count):
+            dst = y_turned[h][:].bitcast(F32)[:, 2 * t0 * P:2 * (t0 + count) * P]
+            nc.scalar.copy(
+                out=dst.rearrange("p (j m e) -> p j m e", j=count, e=2),
+                in_=turn[h, t0][:].rearrange("p j e m -> p j m e"),
+            )
+
+        def quantise_y(h, t0, count):
+            nc.vector.quantize_mx(
+                out=y_code[h][:, users(t0, count)].bitcast(FP8X4),
+                scales=y_scale[h][:, users(t0, count)],
+                in_=y_turned[h][:, PACK * t0 * P:PACK * (t0 + count) * P],
+            )
+
+        def store_y(h, t):
+            nc.sync.dma_start(out=out_0[users(t), half(h)], in_=y_sb[h, t][:])
+
+        def store_codes(h, t0, count):
+            dst = out_1[h].rearrange("p m t -> p (m t)").bitcast(I32)
+            nc.sync.dma_start(out=dst[:, users(t0, count)], in_=y_code[h][:, users(t0, count)].bitcast(I32))
+
+        def store_scales(h, q, queue):
+            queue.dma_start(out=out_2[h, scale_rows(q), :].bitcast(I32), in_=y_scale[h][live(q), :].bitcast(I32))
+
+        for t in range(TILES):
+            acc_b[0, t] = bank(t, "acc_b0_%d" % t, [P, HALF])
+        for g in range(PASSES):
+            for t in range(TILES):
+                pass_b(acc_b[0, t], 0, t, g)
+        for t in range(2):
+            acc_b[1, t] = bank(6 + t, "acc_b1_%d" % t, [P, HALF])
+        for g in range(PASSES):
+            for t in range(2):
+                pass_b(acc_b[1, t], 1, t, g)
+        for t in range(TILES):
+            weigh(0, t)
+        for t in range(2):
+            weigh(1, t)
+        for t in range(2, TILES):
+            acc_b[1, t] = bank(t - 2, "acc_b1_%d" % t, [P, HALF])
+            for g in range(PASSES):
+                pass_b(acc_b[1, t], 1, t, g)
+            weigh(1, t)
+        for t in range(TILES):
+            acc_ad[0, t] = bank((4 + t) % 8, "acc_ad0_%d" % t, [P, HALF])
+        for g in range(PASSES):
+            for t in range(TILES):
+                pass_a(acc_ad[0, t], 0, t, g)
+        for t in range(2):
+            acc_ad[1, t] = bank(2 + t, "acc_ad1_%d" % t, [P, HALF])
+            for g in range(PASSES):
+                pass_a(acc_ad[1, t], 1, t, g)
+        interleave_d(0, 0, False)
+        quantise_d(0, 0)
+        interleave_d(1, 0, False)
+        interleave_d(1, 1, True)
+        quantise_d(1, 0)
+        quantise_d(1, 1)
+        interleave_d(0, 1, False)
+        interleave_d(1, 2, True)
+        quantise_d(0, 1)
+        quantise_d(1, 2)
+        interleave_d(0, 2, False)
+        interleave_d(1, 3, True)
+        quantise_d(0, 2)
+        quantise_d(1, 3)
+        interleave_d(0, 3, False)
+        subtract_from_x(0, 0)
+        subtract_from_x(0, 1)
+        quantise_d(0, 3)
+        for g in range(PASSES):
+            for t in range(TILES):
+                pass_d(acc_ad[0, t], 0, t, g)
+        for t in range(TILES):
+            if t + 2 < TILES:
+                subtract_from_x(0, t + 2)
+            finish(0, t)
+            store_y(0, t)
+            round_y(0, t)
+        for t in range(2):
+            for g in range(PASSES):
+                pass_d(acc_ad[1, t], 1, t, g)
+
+        def product_ad(t, bank_index):
+            acc_ad[1, t] = bank(bank_index, "acc_ad1_%d" % t, [P, HALF])
+            for g in range(PASSES):
+                pass_a(acc_ad[1, t], 1, t, g)
+            for g in range(PASSES):
+                pass_d(acc_ad[1, t], 1, t, g)
+
+        product_ad(2, 4)
+        product_ad(3, 5)
+        for t in range(2):
+            subtract_from_x(1, t)
+        for t in range(2):
+            finish(1, t)
+            store_y(1, t)
+            round_y(1, t)
+        transpose_y(0, 0, 2, 6)
+        transpose_y(0, 2, 2, 7)
+        transpose_y(0, 4, 2, 0)
+        copy_turned(0, 0, 2)
+        copy_turned(0, 2, 2)
+        for t in range(2, 4):
+            subtract_from_x(1, t)
+        for t in range(2, 4):
+            finish(1, t)
+            store_y(1, t)
+            round_y(1, t)
+        copy_turned(0, 4, 2)
+        product_ad(4, 1)
+        for t in range(4, 6):
+            subtract_from_x(1, t)
+        quantise_y(0, 0, 4)
+        finish(1, 4)
+        quantise_y(0, 4, 2)
+        store_codes(0, 0, TILES)
+        for q in range(QUADRANTS):
+            store_scales(0, q, nc.sync)
+        store_y(1, 4)
+        transpose_y(1, 0, 2, 2)
+        transpose_y(1, 2, 2, 3)
+        copy_turned(1, 0, 2)
+        copy_turned(1, 2, 2)
+        round_y(1, 4)
+        product_ad(5, 4)
+        quantise_y(1, 0, 4)
+        store_codes(1, 0, 4)
+        transpose_y(1, 4, 1, 5)
+        copy_turned(1, 4, 1)
+        finish_rounded(1, 5)
+        finish(1, 5)
+        store_y(1, 5)
+        transpose_y(1, 5, 1, 6)
+        copy_turned(1, 5, 1)
+        quantise_y(1, 4, 2)
+        store_codes(1, 4, 2)
+        for q in range(QUADRANTS):
+            store_scales(1, q, nc.sync if q < 2 else nc.scalar)

@@ -25,6 +25,7 @@ HALF = 512
 HALVES = FACTORS // HALF
 QUADRANTS = 4
 ALIGN = 256
+WARM_PASSES = 18
 
 
 def tile_implicit_als_user_gradient_k3_kernel(
@@ -43,10 +44,15 @@ def tile_implicit_als_user_gradient_k3_kernel(
             return psum.tile(shape, F32, name=name, tag="bank%d" % index)
 
         e_code = [sb("e_code%d" % g, [P, USERS], U32) for g in range(PASSES)]
-        e_scale_first = sb("e_scale_first", [P, USERS], U8)
-        e_scale_rest = sb("e_scale_rest", [P, PASSES - 1, USERS], U8)
+        first_scales = sb("first_scales", [P, USERS + HALF], U8)
+        e_packed = first_scales[:, :USERS]
+        e_scale = sb("e_scale", [P, PASSES, USERS], U8)
         b_code = [[sb("b_code%d_%d" % (h, g), [P, HALF], U32) for g in range(PASSES)] for h in range(HALVES)]
-        b_scale = sb("b_scale", [P, FACTORS], U8)
+        b_packed_late = sb("b_packed_late", [P, HALF], U8)
+        b_packed = [first_scales[:, USERS:], b_packed_late[:]]
+        warm_in = sb("warm_in", [P, PACK * P], BF16)
+        warm_code = sb("warm_code", [P, P], U32)
+        warm_scale = sb("warm_scale", [P, P], U8)
         a_code = [sb("a_code%d" % g, [P, 2 * FACTORS], U8) for g in range(PASSES)]
         a_scale = sb("a_scale", [P, PASSES, FACTORS], U8)
         d_raw = [sb("d_raw%d" % g, [P, PACK, FACTORS], BF16) for g in range(PASSES)]
@@ -84,19 +90,16 @@ def tile_implicit_als_user_gradient_k3_kernel(
             src = b_words[g].rearrange("p n t -> p (n t)").bitcast(I32)
             load(b_code[h][g][:].bitcast(I32), src[:, half(h)])
 
-        def load_e_scale_first(q):
-            load(e_scale_first[live(q), :].bitcast(I32), e_scales[0, scale_rows(q), :].bitcast(I32))
+        def load_e_packed(q):
+            load(e_packed[live(q, 16), :].bitcast(I32), e_scales[:, scale_rows(q), :].bitcast(I32))
 
-        def load_e_scale_rest(q):
-            src = e_scales[1:PASSES, scale_rows(q), :].rearrange("g r n -> r g n")
-            load(e_scale_rest[live(q), :, :].bitcast(I32), src.bitcast(I32))
+        def load_b_packed(h, q, queue):
+            src = b_scales[:, scale_rows(q), half(h)]
+            queue.dma_start(out=b_packed[h][live(q, 16), :].bitcast(I32), in_=src.bitcast(I32))
 
-        def load_b_scale(q):
-            load(b_scale[live(q, 16), :].bitcast(I32), b_scales[:, scale_rows(q), :].bitcast(I32))
-
-        def load_a_scale(q):
-            src = a_scales[:, scale_rows(q), :].rearrange("g r n -> r g n")
-            load(a_scale[live(q), :, :].bitcast(I32), src.bitcast(I32))
+        def load_plain_scales(dst, scales, q):
+            src = scales[:, scale_rows(q), :].rearrange("g r n -> r g n")
+            nc.gpsimd.dma_start(out=dst[live(q), :, :].bitcast(I32), in_=src.bitcast(I32))
 
         def load_a(g):
             load(a_code[g][:].bitcast(I32), a_words[g].bitcast(I32))
@@ -104,33 +107,50 @@ def tile_implicit_als_user_gradient_k3_kernel(
         def load_d(g):
             load(d_raw[g][:], d[g * K_PASS:(g + 1) * K_PASS, :].rearrange("(p j) f -> p j f", j=PACK))
 
-        nc.vector.memset(e_scale_first[:].bitcast(I32), 0)
-        nc.vector.memset(b_scale[:].bitcast(I32), 0)
-        nc.vector.memset(e_scale_rest[:].bitcast(I32), 0)
+        nc.vector.memset(first_scales[:].bitcast(I32), 0)
+        nc.vector.memset(warm_in[:], 1.0)
+        nc.vector.memset(b_packed_late[:].bitcast(I32), 0)
+        nc.vector.quantize_mx(out=warm_code[:].bitcast(FP8X4), scales=warm_scale[:], in_=warm_in[:])
+        nc.vector.memset(e_scale[:].bitcast(I32), 0)
         nc.vector.memset(a_scale[:].bitcast(I32), 0)
         nc.vector.memset(ident[:], 0.0)
+
+        for q in (0, 2, 1, 3):
+            load_plain_scales(e_scale, e_scales, q)
+        for q in (0, 2, 1, 3):
+            load_plain_scales(a_scale, a_scales, q)
         make_identity(nc, ident[:], nomemset=True)
 
-        load_e_scale_first(0)
-        load_e_scale_first(2)
-        load_b(0, 0)
+        warm_out = bank(7, "warm_out", [P, 4, P])
+        for i in range(WARM_PASSES):
+            nc.tensor.matmul_mx(
+                out=warm_out[:, i % 4, :],
+                lhsT=warm_code[:].bitcast(FP8X4),
+                lhsT_scale=warm_scale[:],
+                rhs=warm_code[:].bitcast(FP8X4),
+                rhs_scale=warm_scale[:],
+                start=True,
+                stop=True,
+            )
+
         load_e(0, 0, 3)
-        load_e_scale_first(1)
-        load_e_scale_first(3)
-        for q in range(QUADRANTS):
-            load_b_scale(q)
+        load_b(0, 0)
+        for q in (0, 2, 1, 3):
+            load_e_packed(q)
         load_e(0, 3, 3)
-        for q in range(QUADRANTS):
-            load_e_scale_rest(q)
-        for g in range(1, PASSES):
+        load_b(0, 1)
+        for q in (0, 2, 1, 3):
+            load_b_packed(0, q, nc.sync)
+        load_e(1, 0, TILES)
+        for g in range(2, PASSES):
             load_b(0, g)
             load_e(g, 0, TILES)
+        for q in (0, 2, 1, 3):
+            load_b_packed(1, q, nc.sync)
         for g in range(PASSES):
             load_b(1, g)
         for t in range(TILES):
             load(gain_sb[t][:], gain[users(t), :])
-        for q in range(QUADRANTS):
-            load_a_scale(q)
         load_a(0)
         load_d(0)
         for g in range(1, PASSES):
@@ -140,12 +160,11 @@ def tile_implicit_als_user_gradient_k3_kernel(
         for t in range(TILES):
             load(x_sb[t][:], x[users(t), :])
 
-        def mx_pass(acc, t, g, rhs, rhs_scale, start, stop):
-            e_scale = e_scale_first[:, users(t)] if g == 0 else e_scale_rest[:, g - 1, users(t)]
+        def mx_pass(acc, t, g, lhs_scale, rhs, rhs_scale, start, stop):
             nc.tensor.matmul_mx(
                 out=acc[:],
                 lhsT=e_code[g][:, users(t)].bitcast(FP8X4),
-                lhsT_scale=e_scale,
+                lhsT_scale=lhs_scale,
                 rhs=rhs,
                 rhs_scale=rhs_scale,
                 start=start,
@@ -153,14 +172,16 @@ def tile_implicit_als_user_gradient_k3_kernel(
             )
 
         def pass_b(acc, h, t, g):
-            mx_pass(acc, t, g, b_code[h][g][:].bitcast(FP8X4), b_scale[4 * g:P, half(h)], g == 0, g == PASSES - 1)
+            rhs = b_code[h][g][:].bitcast(FP8X4)
+            mx_pass(acc, t, g, e_packed[4 * g:P, users(t)], rhs, b_packed[h][4 * g:P, :], g == 0, g == PASSES - 1)
 
         def pass_a(acc, h, t, g):
             rhs = a_code[g][:, 2 * h * HALF:2 * (h + 1) * HALF].bitcast(FP4X4)
-            mx_pass(acc, t, g, rhs, a_scale[:, g, half(h)], g == 0, False)
+            mx_pass(acc, t, g, e_scale[:, g, users(t)], rhs, a_scale[:, g, half(h)], g == 0, False)
 
         def pass_d(acc, h, t, g):
-            mx_pass(acc, t, g, d_code[h][g][:].bitcast(FP8X4), d_scale[h][g][:], False, g == PASSES - 1)
+            rhs = d_code[h][g][:].bitcast(FP8X4)
+            mx_pass(acc, t, g, e_scale[:, g, users(t)], rhs, d_scale[h][g][:], False, g == PASSES - 1)
 
         grouped = {}
 

@@ -14,6 +14,7 @@ U8 = mybir.dt.uint8
 FP8X4 = mybir.dt.float8_e4m3fn_x4
 FP4X4 = mybir.dt.float4_e2m1fn_x4
 MULT = mybir.AluOpType.mult
+ADD = mybir.AluOpType.add
 SUBTRACT = mybir.AluOpType.subtract
 
 P = 128
@@ -46,16 +47,17 @@ def tile_implicit_als_user_gradient_k3_kernel(
         e_code = [sb("e_code%d" % g, [P, USERS], U32) for g in range(PASSES)]
         first_scales = sb("first_scales", [P, USERS + HALF], U8)
         e_packed = first_scales[:, :USERS]
-        e_scale = sb("e_scale", [P, PASSES, USERS], U8)
-        b_code = [[sb("b_code%d_%d" % (h, g), [P, HALF], U32) for g in range(PASSES)] for h in range(HALVES)]
+        b_code = [
+            [sb("b_code%d_%d" % (h, g), [P, HALF], U32, tag="b_slot%d_%d" % (h, g)) for g in range(PASSES)]
+            for h in range(HALVES)
+        ]
         b_packed_late = sb("b_packed_late", [P, HALF], U8)
         b_packed = [first_scales[:, USERS:], b_packed_late[:]]
         warm_in = sb("warm_in", [P, PACK * P], BF16)
-        warm_code = sb("warm_code", [P, P], U32)
+        warm_code = sb("warm_code", [P, P], U32, tag="warm_slot")
         warm_scale = sb("warm_scale", [P, P], U8)
         a_code = [sb("a_code%d" % g, [P, 2 * FACTORS], U8) for g in range(PASSES)]
-        a_scale = sb("a_scale", [P, PASSES, FACTORS], U8)
-        d_raw = [sb("d_raw%d" % g, [P, PACK, FACTORS], BF16) for g in range(PASSES)]
+        d_raw = {}
         d_code = [[sb("d_code%d_%d" % (h, g), [P, HALF], U32) for g in range(PASSES)] for h in range(HALVES)]
         d_scale = [[sb("d_scale%d_%d" % (h, g), [P, HALF], U8) for g in range(PASSES)] for h in range(HALVES)]
         gain_sb = [sb("gain%d" % t, [P, FACTORS], BF16) for t in range(TILES)]
@@ -101,24 +103,29 @@ def tile_implicit_als_user_gradient_k3_kernel(
             src = scales[:, scale_rows(q), :].rearrange("g r n -> r g n")
             nc.gpsimd.dma_start(out=dst[live(q), :, :].bitcast(I32), in_=src.bitcast(I32))
 
-        def load_a(g):
-            load(a_code[g][:].bitcast(I32), a_words[g].bitcast(I32))
+        def load_a(g, h0, count):
+            cols = slice(h0 * HALF // 2, (h0 + count) * HALF // 2)
+            load(a_code[g][:].bitcast(I32)[:, cols], a_words[g].bitcast(I32)[:, cols])
 
-        def load_d(g):
-            load(d_raw[g][:], d[g * K_PASS:(g + 1) * K_PASS, :].rearrange("(p j) f -> p j f", j=PACK))
+        def load_d(g, h0, count):
+            cols = slice(h0 * HALF, (h0 + count) * HALF)
+            rows = d[g * K_PASS:(g + 1) * K_PASS, cols]
+            dst = sb("d_raw%d_%d" % (h0, g), [P, PACK, count * HALF], BF16)
+            for j in range(count):
+                d_raw[h0 + j, g] = dst[:, :, half(j)]
+            load(dst[:], rows.rearrange("(p j) f -> p j f", j=PACK))
+
+        def load_gain(t):
+            load(gain_sb[t][:], gain[users(t), :])
+
+        def load_x(t):
+            load(x_sb[t][:], x[users(t), :])
 
         nc.vector.memset(first_scales[:].bitcast(I32), 0)
         nc.vector.memset(warm_in[:], 1.0)
         nc.vector.memset(b_packed_late[:].bitcast(I32), 0)
         nc.vector.quantize_mx(out=warm_code[:].bitcast(FP8X4), scales=warm_scale[:], in_=warm_in[:])
-        nc.vector.memset(e_scale[:].bitcast(I32), 0)
-        nc.vector.memset(a_scale[:].bitcast(I32), 0)
         nc.vector.memset(ident[:], 0.0)
-
-        for q in (0, 2, 1, 3):
-            load_plain_scales(e_scale, e_scales, q)
-        for q in (0, 2, 1, 3):
-            load_plain_scales(a_scale, a_scales, q)
         make_identity(nc, ident[:], nomemset=True)
 
         warm_out = bank(7, "warm_out", [P, 4, P])
@@ -149,16 +156,24 @@ def tile_implicit_als_user_gradient_k3_kernel(
             load_b_packed(1, q, nc.sync)
         for g in range(PASSES):
             load_b(1, g)
-        for t in range(TILES):
-            load(gain_sb[t][:], gain[users(t), :])
-        load_a(0)
-        load_d(0)
-        for g in range(1, PASSES):
-            load_a(g)
-        for g in range(1, PASSES):
-            load_d(g)
-        for t in range(TILES):
-            load(x_sb[t][:], x[users(t), :])
+        for t in range(4):
+            load_gain(t)
+        load_a(0, 0, 2)
+        load_gain(4)
+        load_gain(5)
+        load_a(1, 0, 2)
+        load_a(2, 0, 2)
+        load_a(3, 0, 2)
+        load_d(0, 0, 2)
+        load_d(1, 0, 2)
+        load_d(2, 0, 1)
+        load_d(3, 0, 1)
+        for t in range(3):
+            load_x(t)
+        load_d(2, 1, 1)
+        load_d(3, 1, 1)
+        for t in range(3, TILES):
+            load_x(t)
 
         def mx_pass(acc, t, g, lhs_scale, rhs, rhs_scale, start, stop):
             nc.tensor.matmul_mx(
@@ -177,22 +192,32 @@ def tile_implicit_als_user_gradient_k3_kernel(
 
         def pass_a(acc, h, t, g):
             rhs = a_code[g][:, 2 * h * HALF:2 * (h + 1) * HALF].bitcast(FP4X4)
-            mx_pass(acc, t, g, e_scale[:, g, users(t)], rhs, a_scale[:, g, half(h)], g == 0, False)
+            lhs_scale = e_packed[:, users(t)] if g == 0 else plain["e"][:, g - 1, users(t)]
+            mx_pass(acc, t, g, lhs_scale, rhs, plain["a"][:, g, half(h)], g == 0, False)
 
         def pass_d(acc, h, t, g):
             rhs = d_code[h][g][:].bitcast(FP8X4)
-            mx_pass(acc, t, g, e_scale[:, g, users(t)], rhs, d_scale[h][g][:], False, g == PASSES - 1)
+            mx_pass(acc, t, g, e_packed[4 * g:P, users(t)], rhs, d_scale[h][g][:], False, g == PASSES - 1)
+
+        plain = {}
+
+        def fetch_plain_scales(key, scales, slot):
+            plain[key] = sb(key + "_scale", [P, scales.shape[0], scales.shape[2]], U8, tag=slot)
+            nc.vector.memset(plain[key][:].bitcast(I32), 0)
+            for q in (0, 2, 1, 3):
+                load_plain_scales(plain[key], scales, q)
 
         grouped = {}
 
         def interleave_d(h, g, on_vector):
             dst = sb("d_grouped%d_%d" % (h, g), [P, HALF, PACK], BF16, tag="d_grouped", bufs=4)
             grouped[h, g] = dst
-            src = d_raw[g][:, :, half(h)].rearrange("p j c -> p c j")
+            src = d_raw[h, g].rearrange("p j (c i) -> p c j i", i=4)
+            dst_view = dst[:].rearrange("p (c i) j -> p c j i", i=4)
             if on_vector:
-                nc.vector.tensor_copy(out=dst[:], in_=src)
+                nc.vector.tensor_copy(out=dst_view, in_=src)
             else:
-                nc.scalar.copy(out=dst[:], in_=src)
+                nc.scalar.copy(out=dst_view, in_=src)
 
         def quantise_d(h, g):
             nc.vector.quantize_mx(
@@ -212,6 +237,13 @@ def tile_implicit_als_user_gradient_k3_kernel(
         def finish(h, t):
             y_sb[h, t] = sb("y%d_%d" % (h, t), [P, HALF], F32, tag="y", bufs=TILES)
             nc.vector.tensor_tensor(out=y_sb[h, t][:], in0=rest[h][t][:], in1=acc_ad[h, t][:], op=SUBTRACT)
+
+        def add_product(h, t):
+            nc.vector.tensor_tensor(out=rest[h][t][:], in0=acc_ad[h, t][:], in1=rest[h][t][:], op=ADD)
+
+        def finish_from_x(h, t):
+            y_sb[h, t] = sb("y%d_%d" % (h, t), [P, HALF], F32, tag="y", bufs=TILES)
+            nc.vector.tensor_tensor(out=y_sb[h, t][:], in0=x_sb[t][:, half(h)], in1=rest[h][t][:], op=SUBTRACT)
 
         def pair_view(ap):
             return ap.rearrange("u (p e i) -> u e p i", e=2, i=2)
@@ -258,116 +290,135 @@ def tile_implicit_als_user_gradient_k3_kernel(
         def store_scales(h, q, queue):
             queue.dma_start(out=out_2[h, scale_rows(q), :].bitcast(I32), in_=y_scale[h][live(q), :].bitcast(I32))
 
+        def open_bank(accs, h, t, index, name):
+            accs[h, t] = bank(index, "%s%d_%d" % (name, h, t), [P, HALF])
+
+        def all_passes(one_pass, accs, h, t):
+            for g in range(PASSES):
+                one_pass(accs[h, t], h, t, g)
+
         for t in range(TILES):
-            acc_b[0, t] = bank(t, "acc_b0_%d" % t, [P, HALF])
+            open_bank(acc_b, 0, t, t, "acc_b")
         for g in range(PASSES):
             for t in range(TILES):
                 pass_b(acc_b[0, t], 0, t, g)
+        fetch_plain_scales("e", e_scales[1:PASSES], "warm_slot")
+        fetch_plain_scales("a", a_scales, "b_slot0_0")
         for t in range(2):
-            acc_b[1, t] = bank(6 + t, "acc_b1_%d" % t, [P, HALF])
+            open_bank(acc_b, 1, t, 6 + t, "acc_b")
         for g in range(PASSES):
             for t in range(2):
                 pass_b(acc_b[1, t], 1, t, g)
-        for t in range(TILES):
+        for t in range(4):
             weigh(0, t)
         for t in range(2):
             weigh(1, t)
         for t in range(2, TILES):
-            acc_b[1, t] = bank(t - 2, "acc_b1_%d" % t, [P, HALF])
-            for g in range(PASSES):
-                pass_b(acc_b[1, t], 1, t, g)
-            weigh(1, t)
-        for t in range(TILES):
-            acc_ad[0, t] = bank((4 + t) % 8, "acc_ad0_%d" % t, [P, HALF])
+            open_bank(acc_b, 1, t, t - 2, "acc_b")
+            all_passes(pass_b, acc_b, 1, t)
+        weigh(1, 2)
+        weigh(0, 4)
+        weigh(1, 3)
+        weigh(0, 5)
+        weigh(1, 4)
+        weigh(1, 5)
+        for t, index in enumerate((6, 7, 0, 4, 1, 5)):
+            open_bank(acc_ad, 0, t, index, "acc_ad")
         for g in range(PASSES):
             for t in range(TILES):
                 pass_a(acc_ad[0, t], 0, t, g)
         for t in range(2):
-            acc_ad[1, t] = bank(2 + t, "acc_ad1_%d" % t, [P, HALF])
-            for g in range(PASSES):
-                pass_a(acc_ad[1, t], 1, t, g)
-        interleave_d(0, 0, False)
-        quantise_d(0, 0)
+            open_bank(acc_ad, 1, t, 2 + t, "acc_ad")
+            all_passes(pass_a, acc_ad, 1, t)
+        interleave_d(0, 0, True)
         interleave_d(1, 0, False)
-        interleave_d(1, 1, True)
-        quantise_d(1, 0)
-        quantise_d(1, 1)
-        interleave_d(0, 1, False)
-        interleave_d(1, 2, True)
-        quantise_d(0, 1)
-        quantise_d(1, 2)
+        quantise_d(0, 0)
+        interleave_d(0, 1, True)
         interleave_d(0, 2, False)
-        interleave_d(1, 3, True)
+        quantise_d(1, 0)
+        quantise_d(0, 1)
+        interleave_d(0, 3, True)
+        interleave_d(1, 1, False)
         quantise_d(0, 2)
-        quantise_d(1, 3)
-        interleave_d(0, 3, False)
+        quantise_d(0, 3)
         subtract_from_x(0, 0)
         subtract_from_x(0, 1)
-        quantise_d(0, 3)
-        for g in range(PASSES):
+        interleave_d(1, 2, False)
+        for g in range(2):
             for t in range(TILES):
                 pass_d(acc_ad[0, t], 0, t, g)
         for t in range(TILES):
-            if t + 2 < TILES:
-                subtract_from_x(0, t + 2)
-            finish(0, t)
+            for g in range(2, PASSES):
+                pass_d(acc_ad[0, t], 0, t, g)
+        quantise_d(1, 1)
+        interleave_d(1, 3, False)
+        finish(0, 0)
+        subtract_from_x(0, 2)
+        finish(0, 1)
+        finish(0, 2)
+        quantise_d(1, 2)
+        for t in range(3, TILES):
+            add_product(0, t)
+        subtract_from_x(1, 0)
+        quantise_d(1, 3)
+        for t in range(3, TILES):
+            finish_from_x(0, t)
+        for t in range(TILES):
             store_y(0, t)
             round_y(0, t)
+        for t, index in ((2, 6), (3, 7), (4, 0)):
+            open_bank(acc_ad, 1, t, index, "acc_ad")
+            all_passes(pass_a, acc_ad, 1, t)
         for t in range(2):
-            for g in range(PASSES):
-                pass_d(acc_ad[1, t], 1, t, g)
-
-        def product_ad(t, bank_index):
-            acc_ad[1, t] = bank(bank_index, "acc_ad1_%d" % t, [P, HALF])
-            for g in range(PASSES):
-                pass_a(acc_ad[1, t], 1, t, g)
-            for g in range(PASSES):
-                pass_d(acc_ad[1, t], 1, t, g)
-
-        product_ad(2, 4)
-        product_ad(3, 5)
+            all_passes(pass_d, acc_ad, 1, t)
+        subtract_from_x(1, 1)
+        finish(1, 0)
+        subtract_from_x(1, 2)
+        finish(1, 1)
+        all_passes(pass_d, acc_ad, 1, 2)
+        transpose_y(0, 0, 2, 4)
+        transpose_y(0, 2, 2, 1)
+        transpose_y(0, 4, 2, 5)
+        for t in range(3, 5):
+            all_passes(pass_d, acc_ad, 1, t)
+        subtract_from_x(1, 3)
+        finish(1, 2)
         for t in range(2):
-            subtract_from_x(1, t)
-        for t in range(2):
-            finish(1, t)
             store_y(1, t)
             round_y(1, t)
-        transpose_y(0, 0, 2, 6)
-        transpose_y(0, 2, 2, 7)
-        transpose_y(0, 4, 2, 0)
         copy_turned(0, 0, 2)
+        store_y(1, 2)
+        round_y(1, 2)
         copy_turned(0, 2, 2)
-        for t in range(2, 4):
-            subtract_from_x(1, t)
-        for t in range(2, 4):
-            finish(1, t)
-            store_y(1, t)
-            round_y(1, t)
+        subtract_from_x(1, 4)
+        finish(1, 3)
+        store_y(1, 3)
+        round_y(1, 3)
         copy_turned(0, 4, 2)
-        product_ad(4, 1)
-        for t in range(4, 6):
-            subtract_from_x(1, t)
+        subtract_from_x(1, 5)
         quantise_y(0, 0, 4)
         finish(1, 4)
+        store_y(1, 4)
+        round_y(1, 4)
         quantise_y(0, 4, 2)
         store_codes(0, 0, TILES)
         for q in range(QUADRANTS):
             store_scales(0, q, nc.sync)
-        store_y(1, 4)
-        transpose_y(1, 0, 2, 2)
-        transpose_y(1, 2, 2, 3)
+        open_bank(acc_ad, 1, 5, 2, "acc_ad")
+        all_passes(pass_a, acc_ad, 1, 5)
+        transpose_y(1, 0, 2, 3)
+        transpose_y(1, 2, 2, 6)
+        all_passes(pass_d, acc_ad, 1, 5)
         copy_turned(1, 0, 2)
         copy_turned(1, 2, 2)
-        round_y(1, 4)
-        product_ad(5, 4)
-        quantise_y(1, 0, 4)
-        store_codes(1, 0, 4)
-        transpose_y(1, 4, 1, 5)
+        transpose_y(1, 4, 1, 4)
         copy_turned(1, 4, 1)
         finish_rounded(1, 5)
         finish(1, 5)
         store_y(1, 5)
-        transpose_y(1, 5, 1, 6)
+        quantise_y(1, 0, 4)
+        store_codes(1, 0, 4)
+        transpose_y(1, 5, 1, 1)
         copy_turned(1, 5, 1)
         quantise_y(1, 4, 2)
         store_codes(1, 4, 2)

@@ -26,6 +26,7 @@ HALF = 512
 HALVES = FACTORS // HALF
 QUADRANTS = 4
 ALIGN = 256
+VECTOR_SHARE = 352
 WARM_PASSES = 18
 
 
@@ -115,16 +116,27 @@ def tile_implicit_als_user_gradient_k3_kernel(
                 d_raw[h0 + j, g] = dst[:, :, half(j)]
             load(dst[:], rows.rearrange("(p j) f -> p j f", j=PACK))
 
-        def load_gain(t):
-            load(gain_sb[t][:], gain[users(t), :])
+        def load_gain(h, t):
+            load(gain_sb[t][:, half(h)], gain[users(t), half(h)])
 
-        def load_x(t):
-            load(x_sb[t][:], x[users(t), :])
+        def load_x(h, t):
+            load(x_sb[t][:, half(h)], x[users(t), half(h)])
+
+        plain = {}
+
+        def fetch_plain_scales(key, scales, slot):
+            plain[key] = sb(key + "_scale", [P, scales.shape[0], scales.shape[2]], U8, tag=slot)
+            nc.vector.memset(plain[key][:].bitcast(I32), 0)
+            for q in (0, 2, 1, 3):
+                load_plain_scales(plain[key], scales, q)
 
         nc.vector.memset(first_scales[:].bitcast(I32), 0)
         nc.vector.memset(warm_in[:], 1.0)
         nc.vector.memset(b_packed_late[:].bitcast(I32), 0)
         nc.vector.quantize_mx(out=warm_code[:].bitcast(FP8X4), scales=warm_scale[:], in_=warm_in[:])
+        fetch_plain_scales("a0", a_scales[:, :, half(0)], "")
+        plain["e"] = sb("e_scale", [P, PASSES - 1, USERS], U8)
+        nc.vector.memset(plain["e"][:].bitcast(I32), 0)
         nc.vector.memset(ident[:], 0.0)
         make_identity(nc, ident[:], nomemset=True)
 
@@ -152,28 +164,44 @@ def tile_implicit_als_user_gradient_k3_kernel(
         for g in range(2, PASSES):
             load_b(0, g)
             load_e(g, 0, TILES)
+        load_gain(0, 0)
+        load_a(0, 0, 1)
+        for q in (0, 2, 1, 3):
+            src = e_scales[1:PASSES, scale_rows(q), :].rearrange("g r n -> r g n")
+            load(plain["e"][live(q), :, :].bitcast(I32), src.bitcast(I32))
+        load_a(1, 0, 1)
+        load_gain(0, 1)
+        load_a(2, 0, 1)
+        load_a(3, 0, 1)
+        load_gain(0, 2)
+        load_gain(0, 3)
+        for g in range(PASSES):
+            load_d(g, 0, 1)
+        load_gain(0, 4)
+        load_gain(0, 5)
         for q in (0, 2, 1, 3):
             load_b_packed(1, q, nc.sync)
         for g in range(PASSES):
             load_b(1, g)
-        for t in range(4):
-            load_gain(t)
-        load_a(0, 0, 2)
-        load_gain(4)
-        load_gain(5)
-        load_a(1, 0, 2)
-        load_a(2, 0, 2)
-        load_a(3, 0, 2)
-        load_d(0, 0, 2)
-        load_d(1, 0, 2)
-        load_d(2, 0, 1)
-        load_d(3, 0, 1)
+        load_d(0, 1, 1)
+        load_gain(1, 0)
+        load_gain(1, 1)
+        load_d(1, 1, 1)
         for t in range(3):
-            load_x(t)
+            load_x(0, t)
+        load_gain(1, 2)
+        for g in range(PASSES):
+            load_a(g, 1, 1)
+        for t in range(3, TILES):
+            load_x(0, t)
+        for t in range(3, TILES):
+            load_gain(1, t)
+        load_x(1, 0)
+        load_x(1, 1)
         load_d(2, 1, 1)
         load_d(3, 1, 1)
-        for t in range(3, TILES):
-            load_x(t)
+        for t in range(2, TILES):
+            load_x(1, t)
 
         def mx_pass(acc, t, g, lhs_scale, rhs, rhs_scale, start, stop):
             nc.tensor.matmul_mx(
@@ -193,31 +221,33 @@ def tile_implicit_als_user_gradient_k3_kernel(
         def pass_a(acc, h, t, g):
             rhs = a_code[g][:, 2 * h * HALF:2 * (h + 1) * HALF].bitcast(FP4X4)
             lhs_scale = e_packed[:, users(t)] if g == 0 else plain["e"][:, g - 1, users(t)]
-            mx_pass(acc, t, g, lhs_scale, rhs, plain["a"][:, g, half(h)], g == 0, False)
+            mx_pass(acc, t, g, lhs_scale, rhs, plain["a%d" % h][:, g, :], g == 0, False)
 
         def pass_d(acc, h, t, g):
             rhs = d_code[h][g][:].bitcast(FP8X4)
             mx_pass(acc, t, g, e_packed[4 * g:P, users(t)], rhs, d_scale[h][g][:], False, g == PASSES - 1)
 
-        plain = {}
-
-        def fetch_plain_scales(key, scales, slot):
-            plain[key] = sb(key + "_scale", [P, scales.shape[0], scales.shape[2]], U8, tag=slot)
-            nc.vector.memset(plain[key][:].bitcast(I32), 0)
-            for q in (0, 2, 1, 3):
-                load_plain_scales(plain[key], scales, q)
-
         grouped = {}
 
-        def interleave_d(h, g, on_vector):
-            dst = sb("d_grouped%d_%d" % (h, g), [P, HALF, PACK], BF16, tag="d_grouped", bufs=4)
-            grouped[h, g] = dst
-            src = d_raw[h, g].rearrange("p j (c i) -> p c j i", i=4)
-            dst_view = dst[:].rearrange("p (c i) j -> p c j i", i=4)
+        def interleave_columns(h, g, first, last, on_vector):
+            src = d_raw[h, g][:, :, first:last].rearrange("p j (c i) -> p c j i", i=4)
+            dst = grouped[h, g][:, first:last, :].rearrange("p (c i) j -> p c j i", i=4)
             if on_vector:
-                nc.vector.tensor_copy(out=dst_view, in_=src)
+                nc.vector.tensor_copy(out=dst, in_=src)
             else:
-                nc.scalar.copy(out=dst_view, in_=src)
+                nc.scalar.copy(out=dst, in_=src)
+
+        def open_grouped(h, g):
+            grouped[h, g] = sb("d_grouped%d_%d" % (h, g), [P, HALF, PACK], BF16, tag="d_grouped", bufs=4)
+
+        def interleave_d(h, g, on_vector):
+            open_grouped(h, g)
+            interleave_columns(h, g, 0, HALF, on_vector)
+
+        def interleave_shared(h, g):
+            open_grouped(h, g)
+            interleave_columns(h, g, 0, VECTOR_SHARE, True)
+            interleave_columns(h, g, VECTOR_SHARE, HALF, False)
 
         def quantise_d(h, g):
             nc.vector.quantize_mx(
@@ -302,115 +332,96 @@ def tile_implicit_als_user_gradient_k3_kernel(
         for g in range(PASSES):
             for t in range(TILES):
                 pass_b(acc_b[0, t], 0, t, g)
-        fetch_plain_scales("e", e_scales[1:PASSES], "warm_slot")
-        fetch_plain_scales("a", a_scales, "b_slot0_0")
         for t in range(2):
-            open_bank(acc_b, 1, t, 6 + t, "acc_b")
+            open_bank(acc_ad, 0, t, 6 + t, "acc_ad")
+        for g in range(PASSES):
+            for t in range(2):
+                pass_a(acc_ad[0, t], 0, t, g)
+        weigh(0, 0)
+        fetch_plain_scales("a1", a_scales[:, :, half(1)], "b_slot0_2")
+        for t in range(1, 4):
+            weigh(0, t)
+        for t in range(2, TILES):
+            open_bank(acc_ad, 0, t, t - 2, "acc_ad")
+            all_passes(pass_a, acc_ad, 0, t)
+        for g in range(PASSES):
+            interleave_shared(0, g)
+            quantise_d(0, g)
+        weigh(0, 4)
+        weigh(0, 5)
+        for g in range(PASSES):
+            for t in range(TILES):
+                pass_d(acc_ad[0, t], 0, t, g)
+        for t in range(2):
+            open_bank(acc_b, 1, t, 4 + t, "acc_b")
         for g in range(PASSES):
             for t in range(2):
                 pass_b(acc_b[1, t], 1, t, g)
-        for t in range(4):
-            weigh(0, t)
-        for t in range(2):
-            weigh(1, t)
-        for t in range(2, TILES):
-            open_bank(acc_b, 1, t, t - 2, "acc_b")
-            all_passes(pass_b, acc_b, 1, t)
-        weigh(1, 2)
-        weigh(0, 4)
-        weigh(1, 3)
-        weigh(0, 5)
-        weigh(1, 4)
-        weigh(1, 5)
-        for t, index in enumerate((6, 7, 0, 4, 1, 5)):
-            open_bank(acc_ad, 0, t, index, "acc_ad")
-        for g in range(PASSES):
-            for t in range(TILES):
-                pass_a(acc_ad[0, t], 0, t, g)
-        for t in range(2):
-            open_bank(acc_ad, 1, t, 2 + t, "acc_ad")
-            all_passes(pass_a, acc_ad, 1, t)
-        interleave_d(0, 0, True)
-        interleave_d(1, 0, False)
-        quantise_d(0, 0)
-        interleave_d(0, 1, True)
-        interleave_d(0, 2, False)
-        quantise_d(1, 0)
-        quantise_d(0, 1)
-        interleave_d(0, 3, True)
-        interleave_d(1, 1, False)
-        quantise_d(0, 2)
-        quantise_d(0, 3)
-        subtract_from_x(0, 0)
-        subtract_from_x(0, 1)
-        interleave_d(1, 2, False)
-        for g in range(2):
-            for t in range(TILES):
-                pass_d(acc_ad[0, t], 0, t, g)
         for t in range(TILES):
-            for g in range(2, PASSES):
-                pass_d(acc_ad[0, t], 0, t, g)
-        quantise_d(1, 1)
-        interleave_d(1, 3, False)
-        finish(0, 0)
-        subtract_from_x(0, 2)
-        finish(0, 1)
-        finish(0, 2)
-        quantise_d(1, 2)
-        for t in range(3, TILES):
             add_product(0, t)
-        subtract_from_x(1, 0)
-        quantise_d(1, 3)
+        for t, index in ((2, 6), (3, 7), (4, 0), (5, 1)):
+            open_bank(acc_b, 1, t, index, "acc_b")
+            all_passes(pass_b, acc_b, 1, t)
+        interleave_d(1, 0, False)
+        interleave_d(1, 1, False)
+        weigh(1, 0)
+        weigh(1, 1)
+        quantise_d(1, 0)
+        for t in range(3):
+            finish_from_x(0, t)
+        weigh(1, 2)
+        quantise_d(1, 1)
         for t in range(3, TILES):
             finish_from_x(0, t)
         for t in range(TILES):
-            store_y(0, t)
             round_y(0, t)
-        for t, index in ((2, 6), (3, 7), (4, 0)):
+        for t in range(3, TILES):
+            weigh(1, t)
+        for t in range(3):
+            open_bank(acc_ad, 1, t, 4 + t, "acc_ad")
+            all_passes(pass_a, acc_ad, 1, t)
+        transpose_y(0, 0, 2, 2)
+        transpose_y(0, 2, 2, 3)
+        transpose_y(0, 4, 2, 1)
+        for t, index in ((3, 7), (4, 0)):
             open_bank(acc_ad, 1, t, index, "acc_ad")
             all_passes(pass_a, acc_ad, 1, t)
-        for t in range(2):
-            all_passes(pass_d, acc_ad, 1, t)
+        for t in range(0, TILES, 2):
+            copy_turned(0, t, 2)
+        subtract_from_x(1, 0)
         subtract_from_x(1, 1)
-        finish(1, 0)
-        subtract_from_x(1, 2)
-        finish(1, 1)
-        all_passes(pass_d, acc_ad, 1, 2)
-        transpose_y(0, 0, 2, 4)
-        transpose_y(0, 2, 2, 1)
-        transpose_y(0, 4, 2, 5)
-        for t in range(3, 5):
-            all_passes(pass_d, acc_ad, 1, t)
-        subtract_from_x(1, 3)
-        finish(1, 2)
-        for t in range(2):
-            store_y(1, t)
-            round_y(1, t)
-        copy_turned(0, 0, 2)
-        store_y(1, 2)
-        round_y(1, 2)
-        copy_turned(0, 2, 2)
-        subtract_from_x(1, 4)
-        finish(1, 3)
-        store_y(1, 3)
-        round_y(1, 3)
-        copy_turned(0, 4, 2)
-        subtract_from_x(1, 5)
+        interleave_d(1, 2, True)
+        interleave_shared(1, 3)
+        quantise_d(1, 2)
+        quantise_d(1, 3)
         quantise_y(0, 0, 4)
-        finish(1, 4)
-        store_y(1, 4)
-        round_y(1, 4)
+        subtract_from_x(1, 2)
         quantise_y(0, 4, 2)
+        for t in range(TILES):
+            store_y(0, t)
         store_codes(0, 0, TILES)
         for q in range(QUADRANTS):
             store_scales(0, q, nc.sync)
+        for g in range(PASSES):
+            for t in range(2):
+                pass_d(acc_ad[1, t], 1, t, g)
+        for t in range(2, 5):
+            all_passes(pass_d, acc_ad, 1, t)
+        for t in range(5):
+            finish(1, t)
+            if t >= 1 and t + 2 < TILES:
+                subtract_from_x(1, t + 2)
+            store_y(1, t)
+            if t < 4:
+                round_y(1, t)
         open_bank(acc_ad, 1, 5, 2, "acc_ad")
         all_passes(pass_a, acc_ad, 1, 5)
         transpose_y(1, 0, 2, 3)
-        transpose_y(1, 2, 2, 6)
+        transpose_y(1, 2, 2, 1)
         all_passes(pass_d, acc_ad, 1, 5)
         copy_turned(1, 0, 2)
         copy_turned(1, 2, 2)
+        round_y(1, 4)
         transpose_y(1, 4, 1, 4)
         copy_turned(1, 4, 1)
         finish_rounded(1, 5)
@@ -418,7 +429,7 @@ def tile_implicit_als_user_gradient_k3_kernel(
         store_y(1, 5)
         quantise_y(1, 0, 4)
         store_codes(1, 0, 4)
-        transpose_y(1, 5, 1, 1)
+        transpose_y(1, 5, 1, 5)
         copy_turned(1, 5, 1)
         quantise_y(1, 4, 2)
         store_codes(1, 4, 2)

@@ -13,8 +13,8 @@ U32 = mybir.dt.uint32
 U8 = mybir.dt.uint8
 FP8X4 = mybir.dt.float8_e4m3fn_x4
 FP4X4 = mybir.dt.float4_e2m1fn_x4
-MULT = mybir.AluOpType.mult
 ADD = mybir.AluOpType.add
+MULT = mybir.AluOpType.mult
 SUBTRACT = mybir.AluOpType.subtract
 
 P = 128
@@ -22,12 +22,17 @@ PACK = 4
 K_PASS = P * PACK
 PASSES = ITEMS // K_PASS
 TILES = USERS // P
+LAST = TILES - 1
 HALF = 512
 HALVES = FACTORS // HALF
-QUADRANTS = 4
+QUADRANT = 32
+SCALE_ROWS = 4
+QUADRANT_ORDER = (0, 2, 1, 3)
 ALIGN = 256
-VECTOR_SHARE = 352
 WARM_PASSES = 18
+VECTOR_SHARE = 352
+INTERLEAVED_BUFS = 4
+Y_BUFS = 8
 
 
 def tile_implicit_als_user_gradient_k3_kernel(
@@ -40,35 +45,13 @@ def tile_implicit_als_user_gradient_k3_kernel(
         ctx.enter_context(tc.manual_schedule())
 
         def sb(name, shape, dtype, tag="", bufs=None):
-            return keep.tile(shape, dtype, name=name, tag=tag, bufs=bufs, align_bytes=ALIGN)
+            return keep.tile(shape, dtype, name=name, tag=tag or name, bufs=bufs, align_bytes=ALIGN)
+
+        def per_half(name, count, shape, dtype):
+            return [[sb("%s%d_%d" % (name, h, i), shape, dtype) for i in range(count)] for h in range(HALVES)]
 
         def bank(index, name, shape):
             return psum.tile(shape, F32, name=name, tag="bank%d" % index)
-
-        e_code = [sb("e_code%d" % g, [P, USERS], U32) for g in range(PASSES)]
-        first_scales = sb("first_scales", [P, USERS + HALF], U8)
-        e_packed = first_scales[:, :USERS]
-        b_code = [
-            [sb("b_code%d_%d" % (h, g), [P, HALF], U32, tag="b_slot%d_%d" % (h, g)) for g in range(PASSES)]
-            for h in range(HALVES)
-        ]
-        b_packed_late = sb("b_packed_late", [P, HALF], U8)
-        b_packed = [first_scales[:, USERS:], b_packed_late[:]]
-        warm_in = sb("warm_in", [P, PACK * P], BF16)
-        warm_code = sb("warm_code", [P, P], U32, tag="warm_slot")
-        warm_scale = sb("warm_scale", [P, P], U8)
-        a_code = [sb("a_code%d" % g, [P, 2 * FACTORS], U8) for g in range(PASSES)]
-        d_raw = {}
-        d_code = [[sb("d_code%d_%d" % (h, g), [P, HALF], U32) for g in range(PASSES)] for h in range(HALVES)]
-        d_scale = [[sb("d_scale%d_%d" % (h, g), [P, HALF], U8) for g in range(PASSES)] for h in range(HALVES)]
-        gain_sb = [sb("gain%d" % t, [P, FACTORS], BF16) for t in range(TILES)]
-        x_sb = [sb("x%d" % t, [P, FACTORS], BF16) for t in range(TILES)]
-        rest = [[sb("rest%d_%d" % (h, t), [P, HALF], F32) for t in range(TILES)] for h in range(HALVES)]
-        y_pairs = [[sb("y_pairs%d_%d" % (h, t), [P, HALF], BF16) for t in range(TILES)] for h in range(HALVES)]
-        y_turned = [sb("y_turned%d" % h, [P, USERS * PACK], BF16) for h in range(HALVES)]
-        y_code = [sb("y_code%d" % h, [P, USERS], U32) for h in range(HALVES)]
-        y_scale = [sb("y_scale%d" % h, [P, USERS], U8) for h in range(HALVES)]
-        ident = sb("ident", [P, P], F32)
 
         def users(t, count=1):
             return slice(t * P, (t + count) * P)
@@ -76,11 +59,36 @@ def tile_implicit_als_user_gradient_k3_kernel(
         def half(h):
             return slice(h * HALF, (h + 1) * HALF)
 
-        def live(q, rows=4):
-            return slice(32 * q, 32 * q + rows)
+        def live(q, passes=1):
+            return slice(QUADRANT * q, QUADRANT * q + SCALE_ROWS * passes)
 
-        def scale_rows(q):
-            return slice(4 * q, 4 * q + 4)
+        def rows_of(q):
+            return slice(SCALE_ROWS * q, SCALE_ROWS * (q + 1))
+
+        e_code = [sb("e_code%d" % g, [P, USERS], U32) for g in range(PASSES)]
+        b_code = per_half("b_code", PASSES, [P, HALF], U32)
+        a_code = per_half("a_code", PASSES, [P, 2 * HALF], U8)
+        d_raw = per_half("d_raw", PASSES, [P, PACK, HALF], BF16)
+        d_code = per_half("d_code", PASSES, [P, HALF], U32)
+        d_scale = per_half("d_scale", PASSES, [P, HALF], U8)
+        first_scales = sb("first_scales", [P, USERS + HALF], U8)
+        b_packed_second = sb("b_packed_second", [P, HALF], U8)
+        e_packed = first_scales[:, :USERS]
+        b_packed = [first_scales[:, USERS:], b_packed_second[:]]
+        e_plain = sb("e_plain", [P, PASSES - 1, USERS], U8)
+        a_plain = {}
+        gain_sb = per_half("gain", TILES, [P, HALF], BF16)
+        x_sb = per_half("x", TILES, [P, HALF], BF16)
+        partial = per_half("partial", TILES, [P, HALF], F32)
+        y_sb = {}
+        y_pairs = per_half("y_pairs", TILES, [P, HALF], BF16)
+        y_turned = [sb("y_turned%d" % h, [P, USERS * PACK], BF16) for h in range(HALVES)]
+        y_code = [sb("y_code%d" % h, [P, USERS], U32) for h in range(HALVES)]
+        y_scale = [sb("y_scale%d" % h, [P, USERS], U8) for h in range(HALVES)]
+        ident = sb("ident", [P, P], F32)
+        warm_in = sb("warm_in", [P, PACK * P], BF16)
+        warm_code = sb("warm_code", [P, P], U32)
+        warm_scale = sb("warm_scale", [P, P], U8)
 
         def load(dst, src):
             nc.sync.dma_start(out=dst, in_=src)
@@ -93,57 +101,48 @@ def tile_implicit_als_user_gradient_k3_kernel(
             src = b_words[g].rearrange("p n t -> p (n t)").bitcast(I32)
             load(b_code[h][g][:].bitcast(I32), src[:, half(h)])
 
-        def load_e_packed(q):
-            load(e_packed[live(q, 16), :].bitcast(I32), e_scales[:, scale_rows(q), :].bitcast(I32))
+        def load_a(h, g):
+            load(a_code[h][g][:].bitcast(I32), a_words[g, :, 2 * h * HALF:2 * (h + 1) * HALF].bitcast(I32))
 
-        def load_b_packed(h, q, queue):
-            src = b_scales[:, scale_rows(q), half(h)]
-            queue.dma_start(out=b_packed[h][live(q, 16), :].bitcast(I32), in_=src.bitcast(I32))
-
-        def load_plain_scales(dst, scales, q):
-            src = scales[:, scale_rows(q), :].rearrange("g r n -> r g n")
-            nc.gpsimd.dma_start(out=dst[live(q), :, :].bitcast(I32), in_=src.bitcast(I32))
-
-        def load_a(g, h0, count):
-            cols = slice(h0 * HALF // 2, (h0 + count) * HALF // 2)
-            load(a_code[g][:].bitcast(I32)[:, cols], a_words[g].bitcast(I32)[:, cols])
-
-        def load_d(g, h0, count):
-            cols = slice(h0 * HALF, (h0 + count) * HALF)
-            rows = d[g * K_PASS:(g + 1) * K_PASS, cols]
-            dst = sb("d_raw%d_%d" % (h0, g), [P, PACK, count * HALF], BF16)
-            for j in range(count):
-                d_raw[h0 + j, g] = dst[:, :, half(j)]
-            load(dst[:], rows.rearrange("(p j) f -> p j f", j=PACK))
+        def load_d(h, g):
+            rows = d[g * K_PASS:(g + 1) * K_PASS, half(h)]
+            load(d_raw[h][g][:], rows.rearrange("(p j) f -> p j f", j=PACK))
 
         def load_gain(h, t):
-            load(gain_sb[t][:, half(h)], gain[users(t), half(h)])
+            load(gain_sb[h][t][:], gain[users(t), half(h)])
 
         def load_x(h, t):
-            load(x_sb[t][:, half(h)], x[users(t), half(h)])
+            load(x_sb[h][t][:], x[users(t), half(h)])
 
-        plain = {}
+        def load_packed(dst, scales, q):
+            load(dst[live(q, PASSES), :].bitcast(I32), scales[:, rows_of(q), :].bitcast(I32))
 
-        def fetch_plain_scales(key, scales, slot):
-            plain[key] = sb(key + "_scale", [P, scales.shape[0], scales.shape[2]], U8, tag=slot)
-            nc.vector.memset(plain[key][:].bitcast(I32), 0)
-            for q in (0, 2, 1, 3):
-                load_plain_scales(plain[key], scales, q)
+        def load_plain(dst, scales, q, queue):
+            src = scales[:, rows_of(q), :].rearrange("g r n -> r g n")
+            queue.dma_start(out=dst[live(q), :, :].bitcast(I32), in_=src.bitcast(I32))
 
-        nc.vector.memset(first_scales[:].bitcast(I32), 0)
+        def clear(scale_tile):
+            nc.vector.memset(scale_tile[:].bitcast(I32), 0)
+
+        def fetch_a_scales(h, tag):
+            a_plain[h] = sb("a_plain%d" % h, [P, PASSES, HALF], U8, tag=tag)
+            clear(a_plain[h])
+            for q in QUADRANT_ORDER:
+                load_plain(a_plain[h], a_scales[:, :, half(h)], q, nc.gpsimd)
+
+        clear(first_scales)
         nc.vector.memset(warm_in[:], 1.0)
-        nc.vector.memset(b_packed_late[:].bitcast(I32), 0)
+        clear(b_packed_second)
         nc.vector.quantize_mx(out=warm_code[:].bitcast(FP8X4), scales=warm_scale[:], in_=warm_in[:])
-        fetch_plain_scales("a0", a_scales[:, :, half(0)], "")
-        plain["e"] = sb("e_scale", [P, PASSES - 1, USERS], U8)
-        nc.vector.memset(plain["e"][:].bitcast(I32), 0)
+        fetch_a_scales(0, "")
+        clear(e_plain)
         nc.vector.memset(ident[:], 0.0)
         make_identity(nc, ident[:], nomemset=True)
 
-        warm_out = bank(7, "warm_out", [P, 4, P])
+        warm_out = bank(7, "warm_out", [P, HALF // P, P])
         for i in range(WARM_PASSES):
             nc.tensor.matmul_mx(
-                out=warm_out[:, i % 4, :],
+                out=warm_out[:, i % (HALF // P), :],
                 lhsT=warm_code[:].bitcast(FP8X4),
                 lhsT_scale=warm_scale[:],
                 rhs=warm_code[:].bitcast(FP8X4),
@@ -152,155 +151,168 @@ def tile_implicit_als_user_gradient_k3_kernel(
                 stop=True,
             )
 
-        load_e(0, 0, 3)
+        load_e(0, 0, TILES // 2)
         load_b(0, 0)
-        for q in (0, 2, 1, 3):
-            load_e_packed(q)
-        load_e(0, 3, 3)
-        load_b(0, 1)
-        for q in (0, 2, 1, 3):
-            load_b_packed(0, q, nc.sync)
-        load_e(1, 0, TILES)
-        for g in range(2, PASSES):
+        for q in QUADRANT_ORDER:
+            load_packed(e_packed, e_scales, q)
+        load_packed(b_packed[0], b_scales[:, :, half(0)], QUADRANT_ORDER[0])
+        load_e(0, TILES // 2, TILES // 2)
+        for q in QUADRANT_ORDER[1:]:
+            load_packed(b_packed[0], b_scales[:, :, half(0)], q)
+        for g in range(1, PASSES):
             load_b(0, g)
             load_e(g, 0, TILES)
         load_gain(0, 0)
-        load_a(0, 0, 1)
-        for q in (0, 2, 1, 3):
-            src = e_scales[1:PASSES, scale_rows(q), :].rearrange("g r n -> r g n")
-            load(plain["e"][live(q), :, :].bitcast(I32), src.bitcast(I32))
-        load_a(1, 0, 1)
+        load_a(0, 0)
+        for q in QUADRANT_ORDER:
+            load_plain(e_plain, e_scales[1:PASSES], q, nc.sync)
+        load_a(0, 1)
         load_gain(0, 1)
-        load_a(2, 0, 1)
-        load_a(3, 0, 1)
+        load_a(0, 2)
+        load_a(0, 3)
         load_gain(0, 2)
         load_gain(0, 3)
         for g in range(PASSES):
-            load_d(g, 0, 1)
+            load_d(0, g)
         load_gain(0, 4)
         load_gain(0, 5)
-        for q in (0, 2, 1, 3):
-            load_b_packed(1, q, nc.sync)
+        for q in QUADRANT_ORDER:
+            load_packed(b_packed[1], b_scales[:, :, half(1)], q)
         for g in range(PASSES):
             load_b(1, g)
-        load_d(0, 1, 1)
+        load_d(1, 0)
         load_gain(1, 0)
         load_gain(1, 1)
-        load_d(1, 1, 1)
+        load_d(1, 1)
         for t in range(3):
             load_x(0, t)
         load_gain(1, 2)
         for g in range(PASSES):
-            load_a(g, 1, 1)
+            load_a(1, g)
         for t in range(3, TILES):
             load_x(0, t)
         for t in range(3, TILES):
             load_gain(1, t)
         load_x(1, 0)
         load_x(1, 1)
-        load_d(2, 1, 1)
-        load_d(3, 1, 1)
+        load_d(1, 2)
+        load_d(1, 3)
         for t in range(2, TILES):
             load_x(1, t)
 
-        def mx_pass(acc, t, g, lhs_scale, rhs, rhs_scale, start, stop):
+        sum_b, sum_ad = {}, {}
+
+        def open_b(h, t, index):
+            sum_b[h, t] = bank(index, "sum_b%d_%d" % (h, t), [P, HALF])
+
+        def open_ad(h, t, index):
+            sum_ad[h, t] = bank(index, "sum_ad%d_%d" % (h, t), [P, HALF])
+
+        def mx_pass(acc, t, g, e_scale, rhs, rhs_scale, start, stop):
             nc.tensor.matmul_mx(
                 out=acc[:],
                 lhsT=e_code[g][:, users(t)].bitcast(FP8X4),
-                lhsT_scale=lhs_scale,
+                lhsT_scale=e_scale,
                 rhs=rhs,
                 rhs_scale=rhs_scale,
                 start=start,
                 stop=stop,
             )
 
-        def pass_b(acc, h, t, g):
+        def pass_b(h, t, g):
+            rows = slice(SCALE_ROWS * g, P)
             rhs = b_code[h][g][:].bitcast(FP8X4)
-            mx_pass(acc, t, g, e_packed[4 * g:P, users(t)], rhs, b_packed[h][4 * g:P, :], g == 0, g == PASSES - 1)
+            mx_pass(sum_b[h, t], t, g, e_packed[rows, users(t)], rhs, b_packed[h][rows, :], g == 0, g == PASSES - 1)
 
-        def pass_a(acc, h, t, g):
-            rhs = a_code[g][:, 2 * h * HALF:2 * (h + 1) * HALF].bitcast(FP4X4)
-            lhs_scale = e_packed[:, users(t)] if g == 0 else plain["e"][:, g - 1, users(t)]
-            mx_pass(acc, t, g, lhs_scale, rhs, plain["a%d" % h][:, g, :], g == 0, False)
+        def pass_a(h, t, g):
+            e_scale = e_packed[:, users(t)] if g == 0 else e_plain[:, g - 1, users(t)]
+            rhs = a_code[h][g][:].bitcast(FP4X4)
+            mx_pass(sum_ad[h, t], t, g, e_scale, rhs, a_plain[h][:, g, :], g == 0, False)
 
-        def pass_d(acc, h, t, g):
+        def pass_d(h, t, g):
+            rows = slice(SCALE_ROWS * g, P)
             rhs = d_code[h][g][:].bitcast(FP8X4)
-            mx_pass(acc, t, g, e_packed[4 * g:P, users(t)], rhs, d_scale[h][g][:], False, g == PASSES - 1)
+            mx_pass(sum_ad[h, t], t, g, e_packed[rows, users(t)], rhs, d_scale[h][g][:], False, g == PASSES - 1)
 
-        grouped = {}
+        def pass_by_pass(one_pass, h, tiles):
+            for g in range(PASSES):
+                for t in tiles:
+                    one_pass(h, t, g)
 
-        def interleave_columns(h, g, first, last, on_vector):
-            src = d_raw[h, g][:, :, first:last].rearrange("p j (c i) -> p c j i", i=4)
-            dst = grouped[h, g][:, first:last, :].rearrange("p (c i) j -> p c j i", i=4)
-            if on_vector:
-                nc.vector.tensor_copy(out=dst, in_=src)
-            else:
-                nc.scalar.copy(out=dst, in_=src)
+        interleaved = {}
 
-        def open_grouped(h, g):
-            grouped[h, g] = sb("d_grouped%d_%d" % (h, g), [P, HALF, PACK], BF16, tag="d_grouped", bufs=4)
+        def interleave_d(h, g, vector_columns):
+            dst = sb("interleaved%d_%d" % (h, g), [P, HALF, PACK], BF16, tag="interleaved", bufs=INTERLEAVED_BUFS)
+            interleaved[h, g] = dst
 
-        def interleave_d(h, g, on_vector):
-            open_grouped(h, g)
-            interleave_columns(h, g, 0, HALF, on_vector)
+            def views(first, last):
+                return dict(
+                    out=dst[:, first:last, :].rearrange("p (c i) j -> p c j i", i=4),
+                    in_=d_raw[h][g][:, :, first:last].rearrange("p j (c i) -> p c j i", i=4),
+                )
 
-        def interleave_shared(h, g):
-            open_grouped(h, g)
-            interleave_columns(h, g, 0, VECTOR_SHARE, True)
-            interleave_columns(h, g, VECTOR_SHARE, HALF, False)
+            if vector_columns > 0:
+                nc.vector.tensor_copy(**views(0, vector_columns))
+            if vector_columns < HALF:
+                nc.scalar.copy(**views(vector_columns, HALF))
 
         def quantise_d(h, g):
             nc.vector.quantize_mx(
                 out=d_code[h][g][:].bitcast(FP8X4),
                 scales=d_scale[h][g][:],
-                in_=grouped[h, g][:].rearrange("p c j -> p (c j)"),
+                in_=interleaved[h, g][:].rearrange("p c j -> p (c j)"),
             )
 
-        acc_b, acc_ad, y_sb, turn = {}, {}, {}, {}
-
         def weigh(h, t):
-            nc.vector.tensor_tensor(out=rest[h][t][:], in0=acc_b[h, t][:], in1=gain_sb[t][:, half(h)], op=MULT)
+            nc.vector.tensor_tensor(out=partial[h][t][:], in0=sum_b[h, t][:], in1=gain_sb[h][t][:], op=MULT)
 
-        def subtract_from_x(h, t):
-            nc.vector.tensor_tensor(out=rest[h][t][:], in0=x_sb[t][:, half(h)], in1=rest[h][t][:], op=SUBTRACT)
+        def new_y(h, t):
+            y_sb[h, t] = sb("y%d_%d" % (h, t), [P, HALF], F32, tag="y", bufs=Y_BUFS)
+            return y_sb[h, t]
 
-        def finish(h, t):
-            y_sb[h, t] = sb("y%d_%d" % (h, t), [P, HALF], F32, tag="y", bufs=TILES)
-            nc.vector.tensor_tensor(out=y_sb[h, t][:], in0=rest[h][t][:], in1=acc_ad[h, t][:], op=SUBTRACT)
+        def add_sum_ad(t):
+            nc.vector.tensor_tensor(out=partial[0][t][:], in0=sum_ad[0, t][:], in1=partial[0][t][:], op=ADD)
 
-        def add_product(h, t):
-            nc.vector.tensor_tensor(out=rest[h][t][:], in0=acc_ad[h, t][:], in1=rest[h][t][:], op=ADD)
+        def finish_first_half(t):
+            nc.vector.tensor_tensor(out=new_y(0, t)[:], in0=x_sb[0][t][:], in1=partial[0][t][:], op=SUBTRACT)
 
-        def finish_from_x(h, t):
-            y_sb[h, t] = sb("y%d_%d" % (h, t), [P, HALF], F32, tag="y", bufs=TILES)
-            nc.vector.tensor_tensor(out=y_sb[h, t][:], in0=x_sb[t][:, half(h)], in1=rest[h][t][:], op=SUBTRACT)
+        def subtract_from_x(t):
+            nc.vector.tensor_tensor(out=partial[1][t][:], in0=x_sb[1][t][:], in1=partial[1][t][:], op=SUBTRACT)
 
-        def pair_view(ap):
+        def finish_second_half(t):
+            nc.vector.tensor_tensor(out=new_y(1, t)[:], in0=partial[1][t][:], in1=sum_ad[1, t][:], op=SUBTRACT)
+
+        turned = {}
+
+        def read_as_pairs(ap):
             return ap.rearrange("u (p e i) -> u e p i", e=2, i=2)
 
         def pairs_out(h, t):
             return y_pairs[h][t][:].rearrange("u (e p i) -> u e p i", e=2, i=2)
 
         def round_y(h, t):
-            nc.scalar.copy(out=pairs_out(h, t), in_=pair_view(y_sb[h, t][:]))
+            nc.scalar.copy(out=pairs_out(h, t), in_=read_as_pairs(y_sb[h, t][:]))
 
-        def finish_rounded(h, t):
+        def finish_last_tile_rounded():
             nc.vector.tensor_tensor(
-                out=pairs_out(h, t), in0=pair_view(rest[h][t][:]), in1=pair_view(acc_ad[h, t][:]), op=SUBTRACT
+                out=pairs_out(1, LAST),
+                in0=read_as_pairs(partial[1][LAST][:]),
+                in1=read_as_pairs(sum_ad[1, LAST][:]),
+                op=SUBTRACT,
             )
 
-        def transpose_y(h, t0, count, bank_index):
-            turn[h, t0] = bank(bank_index, "turn%d_%d" % (h, t0), [P, count, 2, P])
-            for j in range(count):
-                words = y_pairs[h][t0 + j][:].bitcast(F32)
+        def transpose_two_tiles(h, t0, index):
+            turned[h, t0] = bank(index, "turned%d_%d" % (h, t0), [P, 2, 2, P])
+            for j in range(2):
+                pairs = y_pairs[h][t0 + j][:].bitcast(F32)
                 for e in range(2):
-                    nc.tensor.transpose(turn[h, t0][:, j, e, :], words[:, e * P:(e + 1) * P], ident[:])
+                    nc.tensor.transpose(turned[h, t0][:, j, e, :], pairs[:, e * P:(e + 1) * P], ident[:])
 
-        def copy_turned(h, t0, count):
-            dst = y_turned[h][:].bitcast(F32)[:, 2 * t0 * P:2 * (t0 + count) * P]
+        def copy_turned(h, t0):
+            dst = y_turned[h][:].bitcast(F32)[:, 2 * t0 * P:2 * (t0 + 2) * P]
             nc.scalar.copy(
-                out=dst.rearrange("p (j m e) -> p j m e", j=count, e=2),
-                in_=turn[h, t0][:].rearrange("p j e m -> p j m e"),
+                out=dst.rearrange("p (j m e) -> p j m e", j=2, e=2),
+                in_=turned[h, t0][:].rearrange("p j e m -> p j m e"),
             )
 
         def quantise_y(h, t0, count):
@@ -318,120 +330,106 @@ def tile_implicit_als_user_gradient_k3_kernel(
             nc.sync.dma_start(out=dst[:, users(t0, count)], in_=y_code[h][:, users(t0, count)].bitcast(I32))
 
         def store_scales(h, q, queue):
-            queue.dma_start(out=out_2[h, scale_rows(q), :].bitcast(I32), in_=y_scale[h][live(q), :].bitcast(I32))
-
-        def open_bank(accs, h, t, index, name):
-            accs[h, t] = bank(index, "%s%d_%d" % (name, h, t), [P, HALF])
-
-        def all_passes(one_pass, accs, h, t):
-            for g in range(PASSES):
-                one_pass(accs[h, t], h, t, g)
+            queue.dma_start(out=out_2[h, rows_of(q), :].bitcast(I32), in_=y_scale[h][live(q), :].bitcast(I32))
 
         for t in range(TILES):
-            open_bank(acc_b, 0, t, t, "acc_b")
-        for g in range(PASSES):
-            for t in range(TILES):
-                pass_b(acc_b[0, t], 0, t, g)
+            open_b(0, t, t)
+        pass_by_pass(pass_b, 0, range(TILES))
         for t in range(2):
-            open_bank(acc_ad, 0, t, 6 + t, "acc_ad")
-        for g in range(PASSES):
-            for t in range(2):
-                pass_a(acc_ad[0, t], 0, t, g)
+            open_ad(0, t, TILES + t)
+        pass_by_pass(pass_a, 0, range(2))
         weigh(0, 0)
-        fetch_plain_scales("a1", a_scales[:, :, half(1)], "b_slot0_2")
+        fetch_a_scales(1, "b_code0_2")
         for t in range(1, 4):
             weigh(0, t)
         for t in range(2, TILES):
-            open_bank(acc_ad, 0, t, t - 2, "acc_ad")
-            all_passes(pass_a, acc_ad, 0, t)
+            open_ad(0, t, t - 2)
+            pass_by_pass(pass_a, 0, [t])
         for g in range(PASSES):
-            interleave_shared(0, g)
+            interleave_d(0, g, VECTOR_SHARE)
             quantise_d(0, g)
         weigh(0, 4)
         weigh(0, 5)
-        for g in range(PASSES):
-            for t in range(TILES):
-                pass_d(acc_ad[0, t], 0, t, g)
+        pass_by_pass(pass_d, 0, range(TILES))
+
         for t in range(2):
-            open_bank(acc_b, 1, t, 4 + t, "acc_b")
-        for g in range(PASSES):
-            for t in range(2):
-                pass_b(acc_b[1, t], 1, t, g)
+            open_b(1, t, 4 + t)
+        pass_by_pass(pass_b, 1, range(2))
         for t in range(TILES):
-            add_product(0, t)
-        for t, index in ((2, 6), (3, 7), (4, 0), (5, 1)):
-            open_bank(acc_b, 1, t, index, "acc_b")
-            all_passes(pass_b, acc_b, 1, t)
-        interleave_d(1, 0, False)
-        interleave_d(1, 1, False)
+            add_sum_ad(t)
+        for t in range(2, TILES):
+            open_b(1, t, (4 + t) % 8)
+            pass_by_pass(pass_b, 1, [t])
+        interleave_d(1, 0, 0)
+        interleave_d(1, 1, 0)
         weigh(1, 0)
         weigh(1, 1)
         quantise_d(1, 0)
         for t in range(3):
-            finish_from_x(0, t)
+            finish_first_half(t)
         weigh(1, 2)
         quantise_d(1, 1)
         for t in range(3, TILES):
-            finish_from_x(0, t)
+            finish_first_half(t)
         for t in range(TILES):
             round_y(0, t)
         for t in range(3, TILES):
             weigh(1, t)
+
         for t in range(3):
-            open_bank(acc_ad, 1, t, 4 + t, "acc_ad")
-            all_passes(pass_a, acc_ad, 1, t)
-        transpose_y(0, 0, 2, 2)
-        transpose_y(0, 2, 2, 3)
-        transpose_y(0, 4, 2, 1)
-        for t, index in ((3, 7), (4, 0)):
-            open_bank(acc_ad, 1, t, index, "acc_ad")
-            all_passes(pass_a, acc_ad, 1, t)
-        for t in range(0, TILES, 2):
-            copy_turned(0, t, 2)
-        subtract_from_x(1, 0)
-        subtract_from_x(1, 1)
-        interleave_d(1, 2, True)
-        interleave_shared(1, 3)
+            open_ad(1, t, 4 + t)
+            pass_by_pass(pass_a, 1, [t])
+        for t0, index in ((0, 2), (2, 3), (4, 1)):
+            transpose_two_tiles(0, t0, index)
+        for t in range(3, LAST):
+            open_ad(1, t, (4 + t) % 8)
+            pass_by_pass(pass_a, 1, [t])
+        for t0 in range(0, TILES, 2):
+            copy_turned(0, t0)
+        open_ad(1, LAST, 2)
+        for g in range(PASSES // 2):
+            pass_a(1, LAST, g)
+        subtract_from_x(0)
+        subtract_from_x(1)
+        interleave_d(1, 2, HALF)
+        interleave_d(1, 3, VECTOR_SHARE)
         quantise_d(1, 2)
         quantise_d(1, 3)
         quantise_y(0, 0, 4)
-        subtract_from_x(1, 2)
+        subtract_from_x(2)
         quantise_y(0, 4, 2)
         for t in range(TILES):
             store_y(0, t)
         store_codes(0, 0, TILES)
-        for q in range(QUADRANTS):
+        for q in range(len(QUADRANT_ORDER)):
             store_scales(0, q, nc.sync)
-        for g in range(PASSES):
-            for t in range(2):
-                pass_d(acc_ad[1, t], 1, t, g)
-        for t in range(2, 5):
-            all_passes(pass_d, acc_ad, 1, t)
-        for t in range(5):
-            finish(1, t)
-            if t >= 1 and t + 2 < TILES:
-                subtract_from_x(1, t + 2)
+
+        pass_by_pass(pass_d, 1, range(2))
+        for t in range(2, LAST):
+            pass_by_pass(pass_d, 1, [t])
+        for t in range(LAST):
+            finish_second_half(t)
+            if 1 <= t < LAST - 1:
+                subtract_from_x(t + 2)
             store_y(1, t)
-            if t < 4:
-                round_y(1, t)
-        open_bank(acc_ad, 1, 5, 2, "acc_ad")
-        all_passes(pass_a, acc_ad, 1, 5)
-        transpose_y(1, 0, 2, 3)
-        transpose_y(1, 2, 2, 1)
-        all_passes(pass_d, acc_ad, 1, 5)
-        copy_turned(1, 0, 2)
-        copy_turned(1, 2, 2)
-        round_y(1, 4)
-        transpose_y(1, 4, 1, 4)
-        copy_turned(1, 4, 1)
-        finish_rounded(1, 5)
-        finish(1, 5)
-        store_y(1, 5)
-        quantise_y(1, 0, 4)
-        store_codes(1, 0, 4)
-        transpose_y(1, 5, 1, 5)
-        copy_turned(1, 5, 1)
+            round_y(1, t)
+        for g in range(PASSES // 2, PASSES):
+            pass_a(1, LAST, g)
+        pass_by_pass(pass_d, 1, [LAST])
+
+        for t0, index in ((0, 3), (2, 1)):
+            transpose_two_tiles(1, t0, index)
+        for t0 in (0, 2):
+            copy_turned(1, t0)
+        finish_last_tile_rounded()
+        finish_second_half(LAST)
+        store_y(1, LAST)
+        for t0 in (0, 2):
+            quantise_y(1, t0, 2)
+            store_codes(1, t0, 2)
+        transpose_two_tiles(1, 4, 4)
+        copy_turned(1, 4)
         quantise_y(1, 4, 2)
         store_codes(1, 4, 2)
-        for q in range(QUADRANTS):
+        for q in range(len(QUADRANT_ORDER)):
             store_scales(1, q, nc.sync if q < 2 else nc.scalar)

from contextlib import ExitStack

import concourse.mybir as mybir
from concourse.masks import make_identity

USERS, ITEMS, FACTORS = 768, 2048, 1024
FLOPS = 3 * 2 * USERS * ITEMS * FACTORS

F32 = mybir.dt.float32
BF16 = mybir.dt.bfloat16
I32 = mybir.dt.int32
U32 = mybir.dt.uint32
U8 = mybir.dt.uint8
FP8X4 = mybir.dt.float8_e4m3fn_x4
FP4X4 = mybir.dt.float4_e2m1fn_x4
ADD = mybir.AluOpType.add
MULT = mybir.AluOpType.mult
SUBTRACT = mybir.AluOpType.subtract

P = 128
PACK = 4
K_PASS = P * PACK
PASSES = ITEMS // K_PASS
TILES = USERS // P
LAST = TILES - 1
HALF = 512
HALVES = FACTORS // HALF
QUADRANT = 32
SCALE_ROWS = 4
QUADRANT_ORDER = (0, 2, 1, 3)
ALIGN = 256
WARM_PASSES = 18
VECTOR_SHARE = 352
INTERLEAVED_BUFS = 4
Y_BUFS = 8


def tile_implicit_als_user_gradient_k3_kernel(
    tc, e_words, e_scales, a_words, a_scales, b_words, b_scales, d, gain, x, out_0, out_1, out_2
):
    nc = tc.nc
    with ExitStack() as ctx:
        keep = ctx.enter_context(tc.tile_pool(name="keep", bufs=1))
        psum = ctx.enter_context(tc.psum_pool(name="psum", bufs=1))
        ctx.enter_context(tc.manual_schedule())

        def sb(name, shape, dtype, tag="", bufs=None):
            return keep.tile(shape, dtype, name=name, tag=tag or name, bufs=bufs, align_bytes=ALIGN)

        def per_half(name, count, shape, dtype):
            return [[sb("%s%d_%d" % (name, h, i), shape, dtype) for i in range(count)] for h in range(HALVES)]

        def bank(index, name, shape):
            return psum.tile(shape, F32, name=name, tag="bank%d" % index)

        def users(t, count=1):
            return slice(t * P, (t + count) * P)

        def half(h):
            return slice(h * HALF, (h + 1) * HALF)

        def live(q, passes=1):
            return slice(QUADRANT * q, QUADRANT * q + SCALE_ROWS * passes)

        def rows_of(q):
            return slice(SCALE_ROWS * q, SCALE_ROWS * (q + 1))

        e_code = [sb("e_code%d" % g, [P, USERS], U32) for g in range(PASSES)]
        b_code = per_half("b_code", PASSES, [P, HALF], U32)
        a_code = per_half("a_code", PASSES, [P, 2 * HALF], U8)
        d_raw = per_half("d_raw", PASSES, [P, PACK, HALF], BF16)
        d_code = per_half("d_code", PASSES, [P, HALF], U32)
        d_scale = per_half("d_scale", PASSES, [P, HALF], U8)
        first_scales = sb("first_scales", [P, USERS + HALF], U8)
        b_packed_second = sb("b_packed_second", [P, HALF], U8)
        e_packed = first_scales[:, :USERS]
        b_packed = [first_scales[:, USERS:], b_packed_second[:]]
        e_plain = sb("e_plain", [P, PASSES - 1, USERS], U8)
        a_plain = {}
        gain_sb = per_half("gain", TILES, [P, HALF], BF16)
        x_sb = per_half("x", TILES, [P, HALF], BF16)
        partial = per_half("partial", TILES, [P, HALF], F32)
        y_sb = {}
        y_pairs = per_half("y_pairs", TILES, [P, HALF], BF16)
        y_turned = [sb("y_turned%d" % h, [P, USERS * PACK], BF16) for h in range(HALVES)]
        y_code = [sb("y_code%d" % h, [P, USERS], U32) for h in range(HALVES)]
        y_scale = [sb("y_scale%d" % h, [P, USERS], U8) for h in range(HALVES)]
        ident = sb("ident", [P, P], F32)
        warm_in = sb("warm_in", [P, PACK * P], BF16)
        warm_code = sb("warm_code", [P, P], U32)
        warm_scale = sb("warm_scale", [P, P], U8)

        def load(dst, src):
            nc.sync.dma_start(out=dst, in_=src)

        def load_e(g, t0, count):
            src = e_words[g].rearrange("p n t -> p (n t)").bitcast(I32)
            load(e_code[g][:, users(t0, count)].bitcast(I32), src[:, users(t0, count)])

        def load_b(h, g):
            src = b_words[g].rearrange("p n t -> p (n t)").bitcast(I32)
            load(b_code[h][g][:].bitcast(I32), src[:, half(h)])

        def load_a(h, g):
            load(a_code[h][g][:].bitcast(I32), a_words[g, :, 2 * h * HALF:2 * (h + 1) * HALF].bitcast(I32))

        def load_d(h, g):
            rows = d[g * K_PASS:(g + 1) * K_PASS, half(h)]
            load(d_raw[h][g][:], rows.rearrange("(p j) f -> p j f", j=PACK))

        def load_gain(h, t):
            load(gain_sb[h][t][:], gain[users(t), half(h)])

        def load_x(h, t):
            load(x_sb[h][t][:], x[users(t), half(h)])

        def load_packed(dst, scales, q):
            load(dst[live(q, PASSES), :].bitcast(I32), scales[:, rows_of(q), :].bitcast(I32))

        def load_plain(dst, scales, q, queue):
            src = scales[:, rows_of(q), :].rearrange("g r n -> r g n")
            queue.dma_start(out=dst[live(q), :, :].bitcast(I32), in_=src.bitcast(I32))

        def clear(scale_tile):
            nc.vector.memset(scale_tile[:].bitcast(I32), 0)

        def fetch_a_scales(h, tag):
            a_plain[h] = sb("a_plain%d" % h, [P, PASSES, HALF], U8, tag=tag)
            clear(a_plain[h])
            for q in QUADRANT_ORDER:
                load_plain(a_plain[h], a_scales[:, :, half(h)], q, nc.gpsimd)

        clear(first_scales)
        nc.vector.memset(warm_in[:], 1.0)
        clear(b_packed_second)
        nc.vector.quantize_mx(out=warm_code[:].bitcast(FP8X4), scales=warm_scale[:], in_=warm_in[:])
        fetch_a_scales(0, "")
        clear(e_plain)
        nc.vector.memset(ident[:], 0.0)
        make_identity(nc, ident[:], nomemset=True)

        warm_out = bank(7, "warm_out", [P, HALF // P, P])
        for i in range(WARM_PASSES):
            nc.tensor.matmul_mx(
                out=warm_out[:, i % (HALF // P), :],
                lhsT=warm_code[:].bitcast(FP8X4),
                lhsT_scale=warm_scale[:],
                rhs=warm_code[:].bitcast(FP8X4),
                rhs_scale=warm_scale[:],
                start=True,
                stop=True,
            )

        load_e(0, 0, TILES // 2)
        load_b(0, 0)
        for q in QUADRANT_ORDER:
            load_packed(e_packed, e_scales, q)
        load_packed(b_packed[0], b_scales[:, :, half(0)], QUADRANT_ORDER[0])
        load_e(0, TILES // 2, TILES // 2)
        for q in QUADRANT_ORDER[1:]:
            load_packed(b_packed[0], b_scales[:, :, half(0)], q)
        for g in range(1, PASSES):
            load_b(0, g)
            load_e(g, 0, TILES)
        load_gain(0, 0)
        load_a(0, 0)
        for q in QUADRANT_ORDER:
            load_plain(e_plain, e_scales[1:PASSES], q, nc.sync)
        load_a(0, 1)
        load_gain(0, 1)
        load_a(0, 2)
        load_a(0, 3)
        load_gain(0, 2)
        load_gain(0, 3)
        for g in range(PASSES):
            load_d(0, g)
        load_gain(0, 4)
        load_gain(0, 5)
        for q in QUADRANT_ORDER:
            load_packed(b_packed[1], b_scales[:, :, half(1)], q)
        for g in range(PASSES):
            load_b(1, g)
        load_d(1, 0)
        load_gain(1, 0)
        load_gain(1, 1)
        load_d(1, 1)
        for t in range(3):
            load_x(0, t)
        load_gain(1, 2)
        for g in range(PASSES):
            load_a(1, g)
        for t in range(3, TILES):
            load_x(0, t)
        for t in range(3, TILES):
            load_gain(1, t)
        load_x(1, 0)
        load_x(1, 1)
        load_d(1, 2)
        load_d(1, 3)
        for t in range(2, TILES):
            load_x(1, t)

        sum_b, sum_ad = {}, {}

        def open_b(h, t, index):
            sum_b[h, t] = bank(index, "sum_b%d_%d" % (h, t), [P, HALF])

        def open_ad(h, t, index):
            sum_ad[h, t] = bank(index, "sum_ad%d_%d" % (h, t), [P, HALF])

        def mx_pass(acc, t, g, e_scale, rhs, rhs_scale, start, stop):
            nc.tensor.matmul_mx(
                out=acc[:],
                lhsT=e_code[g][:, users(t)].bitcast(FP8X4),
                lhsT_scale=e_scale,
                rhs=rhs,
                rhs_scale=rhs_scale,
                start=start,
                stop=stop,
            )

        def pass_b(h, t, g):
            rows = slice(SCALE_ROWS * g, P)
            rhs = b_code[h][g][:].bitcast(FP8X4)
            mx_pass(sum_b[h, t], t, g, e_packed[rows, users(t)], rhs, b_packed[h][rows, :], g == 0, g == PASSES - 1)

        def pass_a(h, t, g):
            e_scale = e_packed[:, users(t)] if g == 0 else e_plain[:, g - 1, users(t)]
            rhs = a_code[h][g][:].bitcast(FP4X4)
            mx_pass(sum_ad[h, t], t, g, e_scale, rhs, a_plain[h][:, g, :], g == 0, False)

        def pass_d(h, t, g):
            rows = slice(SCALE_ROWS * g, P)
            rhs = d_code[h][g][:].bitcast(FP8X4)
            mx_pass(sum_ad[h, t], t, g, e_packed[rows, users(t)], rhs, d_scale[h][g][:], False, g == PASSES - 1)

        def pass_by_pass(one_pass, h, tiles):
            for g in range(PASSES):
                for t in tiles:
                    one_pass(h, t, g)

        interleaved = {}

        def interleave_d(h, g, vector_columns):
            dst = sb("interleaved%d_%d" % (h, g), [P, HALF, PACK], BF16, tag="interleaved", bufs=INTERLEAVED_BUFS)
            interleaved[h, g] = dst

            def views(first, last):
                return dict(
                    out=dst[:, first:last, :].rearrange("p (c i) j -> p c j i", i=4),
                    in_=d_raw[h][g][:, :, first:last].rearrange("p j (c i) -> p c j i", i=4),
                )

            if vector_columns > 0:
                nc.vector.tensor_copy(**views(0, vector_columns))
            if vector_columns < HALF:
                nc.scalar.copy(**views(vector_columns, HALF))

        def quantise_d(h, g):
            nc.vector.quantize_mx(
                out=d_code[h][g][:].bitcast(FP8X4),
                scales=d_scale[h][g][:],
                in_=interleaved[h, g][:].rearrange("p c j -> p (c j)"),
            )

        def weigh(h, t):
            nc.vector.tensor_tensor(out=partial[h][t][:], in0=sum_b[h, t][:], in1=gain_sb[h][t][:], op=MULT)

        def new_y(h, t):
            y_sb[h, t] = sb("y%d_%d" % (h, t), [P, HALF], F32, tag="y", bufs=Y_BUFS)
            return y_sb[h, t]

        def add_sum_ad(t):
            nc.vector.tensor_tensor(out=partial[0][t][:], in0=sum_ad[0, t][:], in1=partial[0][t][:], op=ADD)

        def finish_first_half(t):
            nc.vector.tensor_tensor(out=new_y(0, t)[:], in0=x_sb[0][t][:], in1=partial[0][t][:], op=SUBTRACT)

        def subtract_from_x(t):
            nc.vector.tensor_tensor(out=partial[1][t][:], in0=x_sb[1][t][:], in1=partial[1][t][:], op=SUBTRACT)

        def finish_second_half(t):
            nc.vector.tensor_tensor(out=new_y(1, t)[:], in0=partial[1][t][:], in1=sum_ad[1, t][:], op=SUBTRACT)

        turned = {}

        def read_as_pairs(ap):
            return ap.rearrange("u (p e i) -> u e p i", e=2, i=2)

        def pairs_out(h, t):
            return y_pairs[h][t][:].rearrange("u (e p i) -> u e p i", e=2, i=2)

        def round_y(h, t):
            nc.scalar.copy(out=pairs_out(h, t), in_=read_as_pairs(y_sb[h, t][:]))

        def finish_last_tile_rounded():
            nc.vector.tensor_tensor(
                out=pairs_out(1, LAST),
                in0=read_as_pairs(partial[1][LAST][:]),
                in1=read_as_pairs(sum_ad[1, LAST][:]),
                op=SUBTRACT,
            )

        def transpose_two_tiles(h, t0, index):
            turned[h, t0] = bank(index, "turned%d_%d" % (h, t0), [P, 2, 2, P])
            for j in range(2):
                pairs = y_pairs[h][t0 + j][:].bitcast(F32)
                for e in range(2):
                    nc.tensor.transpose(turned[h, t0][:, j, e, :], pairs[:, e * P:(e + 1) * P], ident[:])

        def copy_turned(h, t0):
            dst = y_turned[h][:].bitcast(F32)[:, 2 * t0 * P:2 * (t0 + 2) * P]
            nc.scalar.copy(
                out=dst.rearrange("p (j m e) -> p j m e", j=2, e=2),
                in_=turned[h, t0][:].rearrange("p j e m -> p j m e"),
            )

        def quantise_y(h, t0, count):
            nc.vector.quantize_mx(
                out=y_code[h][:, users(t0, count)].bitcast(FP8X4),
                scales=y_scale[h][:, users(t0, count)],
                in_=y_turned[h][:, PACK * t0 * P:PACK * (t0 + count) * P],
            )

        def store_y(h, t):
            nc.sync.dma_start(out=out_0[users(t), half(h)], in_=y_sb[h, t][:])

        def store_codes(h, t0, count):
            dst = out_1[h].rearrange("p m t -> p (m t)").bitcast(I32)
            nc.sync.dma_start(out=dst[:, users(t0, count)], in_=y_code[h][:, users(t0, count)].bitcast(I32))

        def store_scales(h, q, queue):
            queue.dma_start(out=out_2[h, rows_of(q), :].bitcast(I32), in_=y_scale[h][live(q), :].bitcast(I32))

        for t in range(TILES):
            open_b(0, t, t)
        pass_by_pass(pass_b, 0, range(TILES))
        for t in range(2):
            open_ad(0, t, TILES + t)
        pass_by_pass(pass_a, 0, range(2))
        weigh(0, 0)
        fetch_a_scales(1, "b_code0_2")
        for t in range(1, 4):
            weigh(0, t)
        for t in range(2, TILES):
            open_ad(0, t, t - 2)
            pass_by_pass(pass_a, 0, [t])
        for g in range(PASSES):
            interleave_d(0, g, VECTOR_SHARE)
            quantise_d(0, g)
        weigh(0, 4)
        weigh(0, 5)
        pass_by_pass(pass_d, 0, range(TILES))

        for t in range(2):
            open_b(1, t, 4 + t)
        pass_by_pass(pass_b, 1, range(2))
        for t in range(TILES):
            add_sum_ad(t)
        for t in range(2, TILES):
            open_b(1, t, (4 + t) % 8)
            pass_by_pass(pass_b, 1, [t])
        interleave_d(1, 0, 0)
        interleave_d(1, 1, 0)
        weigh(1, 0)
        weigh(1, 1)
        quantise_d(1, 0)
        for t in range(3):
            finish_first_half(t)
        weigh(1, 2)
        quantise_d(1, 1)
        for t in range(3, TILES):
            finish_first_half(t)
        for t in range(TILES):
            round_y(0, t)
        for t in range(3, TILES):
            weigh(1, t)

        for t in range(3):
            open_ad(1, t, 4 + t)
            pass_by_pass(pass_a, 1, [t])
        for t0, index in ((0, 2), (2, 3), (4, 1)):
            transpose_two_tiles(0, t0, index)
        for t in range(3, LAST):
            open_ad(1, t, (4 + t) % 8)
            pass_by_pass(pass_a, 1, [t])
        for t0 in range(0, TILES, 2):
            copy_turned(0, t0)
        open_ad(1, LAST, 2)
        for g in range(PASSES // 2):
            pass_a(1, LAST, g)
        subtract_from_x(0)
        subtract_from_x(1)
        interleave_d(1, 2, HALF)
        interleave_d(1, 3, VECTOR_SHARE)
        quantise_d(1, 2)
        quantise_d(1, 3)
        quantise_y(0, 0, 4)
        subtract_from_x(2)
        quantise_y(0, 4, 2)
        for t in range(TILES):
            store_y(0, t)
        store_codes(0, 0, TILES)
        for q in range(len(QUADRANT_ORDER)):
            store_scales(0, q, nc.sync)

        pass_by_pass(pass_d, 1, range(2))
        for t in range(2, LAST):
            pass_by_pass(pass_d, 1, [t])
        for t in range(LAST):
            finish_second_half(t)
            if 1 <= t < LAST - 1:
                subtract_from_x(t + 2)
            store_y(1, t)
            round_y(1, t)
        for g in range(PASSES // 2, PASSES):
            pass_a(1, LAST, g)
        pass_by_pass(pass_d, 1, [LAST])

        for t0, index in ((0, 3), (2, 1)):
            transpose_two_tiles(1, t0, index)
        for t0 in (0, 2):
            copy_turned(1, t0)
        finish_last_tile_rounded()
        finish_second_half(LAST)
        store_y(1, LAST)
        for t0 in (0, 2):
            quantise_y(1, t0, 2)
            store_codes(1, t0, 2)
        transpose_two_tiles(1, 4, 4)
        copy_turned(1, 4)
        quantise_y(1, 4, 2)
        store_codes(1, 4, 2)
        for q in range(len(QUADRANT_ORDER)):
            store_scales(1, q, nc.sync if q < 2 else nc.scalar)
